import numpy as np
import ml_dtypes


def mxq(x, axis, fmt="e4m3"):
    dtype, down = {"e4m3": (ml_dtypes.float8_e4m3fn, 7), "e5m2": (ml_dtypes.float8_e5m2, 14)}[fmt]
    v = np.moveaxis(np.asarray(x, np.float32).astype(ml_dtypes.bfloat16).astype(np.float64), axis, -1)
    blocks = v.reshape(v.shape[:-1] + (-1, 32))
    amax = np.abs(blocks).max(-1, keepdims=True)
    byte = np.maximum(np.where(amax > 0, np.frexp(amax)[1] - 1 + 127, 0) - down, 1)
    scale = np.exp2(byte - 127.0)
    codes = (blocks / scale).astype(np.float32).astype(dtype).astype(np.float64)
    return np.moveaxis((codes * scale).reshape(v.shape), -1, axis)


WIDE = False


def mx_kscale(k):
    if not WIDE:
        return np.ones(k)
    levels = np.array([10, -10, 5, -5, 0])
    if k % 512:
        return np.exp2(np.random.permutation(np.resize(levels, k // 32))).repeat(32)
    a = np.empty((k // 512, 16))
    for p in range(k // 512):
        a[p, :8] = np.random.permutation(np.resize(levels, 8))
        for g in range(8):
            far = levels[np.abs(levels - a[p, g]) >= 10]
            a[p, g + 8] = far[np.random.randint(len(far))]
    return np.exp2(a.ravel()).repeat(32)


BF16 = ml_dtypes.bfloat16


def bf(x):
    return np.asarray(x, np.float32).astype(BF16)


def f64(x):
    return np.asarray(x).astype(np.float64)

def planes(Y):
    n, m = Y.shape
    b = f64(bf(Y)).reshape(n // 32, 32, m)
    amax = np.abs(b).max(1)
    byte = np.clip(np.where(amax > 0, np.frexp(amax)[1] - 1 + 127 - 7, 1), 1, 254)
    codes = (b * np.exp2(127.0 - byte)[:, None, :]).reshape(n, m).astype(np.float32).astype(ml_dtypes.float8_e4m3fn).view(np.uint8)
    words = codes.reshape(n // 512, 128, 4, m).transpose(0, 1, 3, 2)
    return np.ascontiguousarray(words), np.ascontiguousarray(byte.astype(np.uint8).reshape(n // 512, 16, m))


T, D, S = 2048, 1024, 1024


def sigmoid(v):
    return 1.0 / (1.0 + np.exp(-v))

def setup_inputs():
    s = mx_kscale(T)
    c = np.exp(0.8 * np.random.randn(D))
    x = np.random.randn(T, D) * c[None, :]
    logits = 2.0 * np.random.randn(T, S) - 1.0
    token_weight = np.exp(0.4 * np.random.randn(T))
    slot_scale = 2.0 * np.exp(0.3 * np.random.randn(S)) / np.sqrt(T)
    slot_embed = 0.3 * np.random.randn(D, S) * c[:, None]
    return {
        "x": bf(x / s[:, None]),
        "logits": bf(logits),
        "token_weight": bf(token_weight * s),
        "slot_scale": bf(slot_scale),
        "slot_embed": bf(slot_embed),
    }

def reference(x, logits, token_weight, slot_scale, slot_embed):
    x, logits, token_weight = f64(x), f64(logits), f64(token_weight)
    slot_scale, slot_embed = f64(slot_scale), f64(slot_embed)
    dispatch = sigmoid(logits) * token_weight[:, None]
    xq = mxq(x, 0, "e4m3")
    dq = mxq(dispatch, 0, "e4m3")
    gathered = xq.T @ dq
    y = gathered * slot_scale[None, :] + slot_embed
    Y = y
    words, scales = planes(Y)
    return y, words, scales

@@ -1,0 +1,291 @@
+from contextlib import ExitStack
+
+import concourse.mybir as mybir
+from concourse.masks import make_identity
+
+T, D, S = 2048, 1024, 1024
+FLOPS = 2 * T * D * S
+
+F32 = mybir.dt.float32
+BF16 = mybir.dt.bfloat16
+I32 = mybir.dt.int32
+U32 = mybir.dt.uint32
+U8 = mybir.dt.uint8
+FP8X4 = mybir.dt.float8_e4m3fn_x4
+ACT = mybir.ActivationFunctionType
+ALU = mybir.AluOpType
+
+P = 128
+PACK = 4
+PASS = P * PACK
+PASSES = T // PASS
+HALF = 512
+PAIR = 256
+
+X_VECTOR = [512, 192, 192, 192, 256, 256, 256, 256]
+STEPS = [(0, None), (1, 0), (2, 1), (3, None), (4, None), (5, 2), (6, 3), (7, 4), (None, 5), (None, 6), (None, 7), (None, None), (None, None)]
+Y_VECTOR = [128, 128, 96, 96, 96, 96, 128, 176]
+
+
+def tile_soft_dispatch_expert_inputs_g2_kernel(
+    tc, x, logits, token_weight, slot_scale, slot_embed, out_0, out_1, out_2
+):
+    nc = tc.nc
+    with ExitStack() as ctx:
+        sb = ctx.enter_context(tc.tile_pool(name="sb", bufs=1))
+        ps = ctx.enter_context(tc.psum_pool(name="ps", bufs=1))
+
+        def tiles(name, count, shape, dtype):
+            return [sb.tile(shape, dtype, name="%s%d" % (name, n), align_bytes=64) for n in range(count)]
+
+        banks = [ps.tile([P, 512], F32, name="bank%d" % n) for n in range(8)]
+        ident = sb.tile([P, P], F32, name="ident", align_bytes=64)
+        weight = sb.tile([P, PASSES, PACK], BF16, name="weight", align_bytes=64)
+        scale_raw = sb.tile([P, 8, 2], BF16, name="scale_raw", align_bytes=64)
+        scale = sb.tile([P, 8], F32, name="scale", align_bytes=64)
+        warm = sb.tile([P, 8], F32, name="warm", align_bytes=64)
+        warm_out = sb.tile([P, 8], F32, name="warm_out", align_bytes=64)
+        logit_lo = [None] + tiles("logit_lo", PASSES - 1, [P, PACK, HALF], BF16)
+        logit_hi = sb.tile([P, PASSES, PACK, HALF], BF16, name="logit_hi", align_bytes=64)
+        x_raw = [None] + tiles("x_raw", 2 * PASSES - 1, [P, PACK, HALF], BF16)
+        embed = tiles("embed", 2, [P, PACK, S], BF16)
+        gate = tiles("gate", 2, [P, HALF * PACK], F32)
+        disp = tiles("disp", 2, [P, HALF * PACK], BF16)
+        x_words = tiles("x_words", 3, [P, HALF, PACK], BF16)
+        d_codes = tiles("d_codes", 8, [P, HALF], U32)
+        d_scales = tiles("d_scales", 8, [P, HALF], U8)
+        x_codes = tiles("x_codes", 8, [P, HALF], U32)
+        x_scales = tiles("x_scales", 8, [P, HALF], U8)
+        scaled = tiles("scaled", 4, [P, PACK, P], F32)
+        y = tiles("y", 3, [P, PACK, PAIR], F32)
+        y_words = tiles("y_words", 2, [P, PAIR, PACK], BF16)
+        y_codes = tiles("y_codes", 3, [P, PAIR], U32)
+        y_scales = sb.tile([P, 2, S], U8, name="y_scales", align_bytes=64)
+        logit_head = tiles("logit_head", 2, [P, PACK, PAIR], BF16)
+        x_head = tiles("x_head", 2, [P, PACK, PAIR], BF16)
+
+        ctx.enter_context(tc.manual_schedule())
+
+        def rows(src, k, cols):
+            return src[PASS * k : PASS * (k + 1), cols].rearrange("(p j) w -> p j w", j=PACK)
+
+        with nc.allow_non_contiguous_dma(reason="small per-token and per-slot vectors"):
+            nc.scalar.dma_start(out=weight[:], in_=token_weight.rearrange("(k p j) -> p k j", p=P, j=PACK))
+        nc.vector.memset(warm[:], 0.0)
+        nc.scalar.activation(out=warm_out[:], in_=warm[:], func=ACT.Sigmoid)
+        for h in range(2):
+            cols = slice(PAIR * h, PAIR * (h + 1))
+            nc.sync.dma_start(out=logit_head[h][:], in_=rows(logits, 0, cols))
+            nc.sync.dma_start(out=x_head[h][:], in_=rows(x, 0, cols))
+        for k in range(1, PASSES):
+            nc.sync.dma_start(out=logit_lo[k][:], in_=rows(logits, k, slice(0, HALF)))
+            nc.sync.dma_start(out=x_raw[k][:], in_=rows(x, k, slice(0, HALF)))
+        for k in range(PASSES):
+            nc.sync.dma_start(out=x_raw[PASSES + k][:], in_=rows(x, k, slice(HALF, D)))
+        with nc.allow_non_contiguous_dma(reason="small per-token and per-slot vectors"):
+            nc.sync.dma_start(out=scale_raw[:, :, 0:1], in_=slot_scale.rearrange("(i p o) -> p i o", p=P, o=1))
+        nc.sync.dma_start(out=embed[0][:], in_=rows(slot_embed, 0, slice(0, S)))
+        for k in range(PASSES):
+            nc.sync.dma_start(out=logit_hi[:, k], in_=rows(logits, k, slice(HALF, S)))
+        nc.sync.dma_start(out=embed[1][:], in_=rows(slot_embed, 1, slice(0, S)))
+        make_identity(nc, ident[:])
+
+        def interleave(dst, src, width, on_vector):
+            def views(cols):
+                return (
+                    dst[:, cols, :].rearrange("p (c i) t -> p c t i", i=4),
+                    src[:, :, cols].rearrange("p t (c i) -> p c t i", i=4),
+                )
+
+            def vector_part():
+                if on_vector > 0:
+                    a, b = views(slice(0, on_vector))
+                    nc.vector.tensor_copy(out=a, in_=b)
+
+            def scalar_part():
+                if on_vector < width:
+                    a, b = views(slice(on_vector, width))
+                    nc.scalar.copy(out=a, in_=b)
+
+            return vector_part, scalar_part
+
+        def x_parts(u):
+            return interleave(x_words[u % 3], x_raw[u], HALF, X_VECTOR[u])
+
+        def x_quantize(u):
+            nc.vector.quantize_mx(
+                out=x_codes[u][:].bitcast(FP8X4), scales=x_scales[u][:],
+                in_=x_words[u % 3][:].rearrange("p c t -> p (c t)"))
+
+        def sigmoid(u):
+            if u < PASSES:
+                nc.scalar.activation(
+                    out=gate[u % 2][:].rearrange("p (s j) -> p s j", j=PACK),
+                    in_=logit_lo[u][:].rearrange("p j s -> p s j"), func=ACT.Sigmoid)
+            else:
+                cols = slice(P * (u - 4), P * (u - 3))
+                nc.scalar.activation(
+                    out=gate[u % 2][:].rearrange("p (k s j) -> p k s j", k=PASSES, j=PACK),
+                    in_=logit_hi[:, :, :, cols].rearrange("p k j s -> p k s j"), func=ACT.Sigmoid)
+
+        def weigh(u):
+            if u < PASSES:
+                nc.vector.tensor_tensor(
+                    out=disp[u % 2][:].rearrange("p (s j) -> p s j", j=PACK),
+                    in0=gate[u % 2][:].rearrange("p (s j) -> p s j", j=PACK),
+                    in1=weight[:, u : u + 1, :].to_broadcast([P, HALF, PACK]), op=ALU.mult)
+            else:
+                nc.vector.tensor_tensor(
+                    out=disp[u % 2][:].rearrange("p (k s j) -> p k s j", k=PASSES, j=PACK),
+                    in0=gate[u % 2][:].rearrange("p (k s j) -> p k s j", k=PASSES, j=PACK),
+                    in1=weight[:].unsqueeze(2).to_broadcast([P, PASSES, P, PACK]), op=ALU.mult)
+
+        def d_quantize(u):
+            nc.vector.quantize_mx(out=d_codes[u][:].bitcast(FP8X4), scales=d_scales[u][:], in_=disp[u % 2][:])
+
+        def bank_of(i, g):
+            if i < 4:
+                return banks[4 * g + i]
+            return banks[4 * ((i - 4) // 2) + 2 * g + i % 2]
+
+        def mx_pass(i, g, k):
+            u, c = (k, i) if i < 4 else (i, k)
+            cols = slice(P * c, P * (c + 1))
+            nc.tensor.matmul_mx(
+                out=bank_of(i, g)[:],
+                lhsT=d_codes[u][:, cols].bitcast(FP8X4), lhsT_scale=d_scales[u][:, cols],
+                rhs=x_codes[PASSES * g + k][:].bitcast(FP8X4), rhs_scale=x_scales[PASSES * g + k][:],
+                start=(k == 0), stop=(k == PASSES - 1))
+
+        def mx_group(i, g):
+            for k in range(PASSES):
+                mx_pass(i, g, k)
+
+        units = [(0, 0), (1, 0), (0, 1), (1, 1), (2, 0), (2, 1), (3, 0), (3, 1)]
+
+        def evacuate(e, h):
+            a, g = units[e]
+            i = 2 * a + h
+            nc.scalar.activation(
+                out=scaled[(2 * e + h) % 4][:],
+                in_=bank_of(i, g)[:].rearrange("p (m t) -> p t m", t=PACK),
+                func=ACT.Copy, scale=scale[:, i : i + 1])
+
+        def turn(e, h):
+            a, g = units[e]
+            for t in range(PACK):
+                nc.tensor.transpose(
+                    bank_of(2 * a + h, g)[:, P * t : P * (t + 1)], scaled[(2 * e + h) % 4][:, t, :], ident[:])
+
+        def add_embed(e, h):
+            a, g = units[e]
+            i = 2 * a + h
+            nc.vector.tensor_tensor(
+                out=y[e % 3][:, :, P * h : P * (h + 1)],
+                in0=bank_of(i, g)[:].rearrange("p (t s) -> p t s", t=PACK),
+                in1=embed[g][:, :, P * i : P * (i + 1)], op=ALU.add)
+
+        def store_y(e):
+            a, g = units[e]
+            nc.sync.dma_start(out=rows(out_0, g, slice(PAIR * a, PAIR * (a + 1))), in_=y[e % 3][:])
+
+        def y_parts(e):
+            return interleave(y_words[e % 2], y[e % 3], PAIR, Y_VECTOR[e])
+
+        def y_quantize(e):
+            a, g = units[e]
+            cols = slice(PAIR * a, PAIR * (a + 1))
+            nc.vector.quantize_mx(
+                out=y_codes[e % 3][:].bitcast(FP8X4), scales=y_scales[:, g, cols],
+                in_=y_words[e % 2][:].rearrange("p c t -> p (c t)"))
+            nc.sync.dma_start(
+                out=out_1[g, :, cols, :].rearrange("p m t -> p (m t)").bitcast(I32),
+                in_=y_codes[e % 3][:].bitcast(I32))
+
+        def store_scales():
+            for q in range(4):
+                queue = nc.sync if q % 2 == 0 else nc.scalar
+                queue.dma_start(
+                    out=out_2[:, 4 * q : 4 * q + 4, :].rearrange("g r s -> r g s").bitcast(I32),
+                    in_=y_scales[32 * q : 32 * q + 4, :, :].bitcast(I32))
+
+        for h in range(2):
+            nc.scalar.activation(
+                out=gate[0][:, PAIR * PACK * h : PAIR * PACK * (h + 1)].rearrange("p (s j) -> p s j", j=PACK),
+                in_=logit_head[h][:].rearrange("p j s -> p s j"), func=ACT.Sigmoid)
+            interleave(x_words[0][:, PAIR * h : PAIR * (h + 1), :], x_head[h], PAIR, PAIR)[0]()
+        for k in range(PASSES):
+            if k > 0:
+                xv, xs = x_parts(k)
+                xv()
+                xs()
+                d_quantize(k - 1)
+                for i in range(4):
+                    mx_pass(i, 0, k - 1)
+            weigh(k)
+            if k + 1 < PASSES:
+                sigmoid(k + 1)
+            x_quantize(k)
+        x_parts(4)[1]()
+        nc.vector.tensor_copy(out=scale[:], in_=scale_raw[:, :, 0])
+        d_quantize(3)
+        for i in range(4):
+            mx_pass(i, 0, 3)
+
+        operands = [("x", 4), ("x", 5), ("x", 6), ("x", 7), ("d", 4), ("d", 5), ("d", 6), ("d", 7)]
+        steps = STEPS
+
+        def scalar_side(kind, u):
+            if kind == "x":
+                x_parts(u)[1]()
+            else:
+                sigmoid(u)
+
+        def vector_side(kind, u):
+            if kind == "x":
+                x_parts(u)[0]()
+            else:
+                weigh(u)
+
+        def finish(kind, u):
+            if kind == "x":
+                x_quantize(u)
+            else:
+                d_quantize(u)
+
+        def multiply(kind, u):
+            if kind == "x":
+                for i in range(4):
+                    mx_pass(i, 1, u - 4)
+            else:
+                mx_group(u, 0)
+                mx_group(u, 1)
+
+        results = [e for (o, e) in steps]
+        for n, (o, e) in enumerate(steps):
+            words = results[n - 1] if n >= 1 else None
+            codes = results[n - 2] if n >= 2 else None
+            if e is not None:
+                evacuate(e, 0)
+                evacuate(e, 1)
+                turn(e, 0)
+                turn(e, 1)
+            if n > 0 and steps[n - 1][0] is not None:
+                multiply(*operands[steps[n - 1][0]])
+            if o is not None:
+                vector_side(*operands[o])
+                if o + 1 < len(operands):
+                    scalar_side(*operands[o + 1])
+            if codes is not None:
+                y_quantize(codes)
+            if words is not None:
+                y_parts(words)[0]()
+                y_parts(words)[1]()
+            if e is not None:
+                add_embed(e, 0)
+            if o is not None:
+                finish(*operands[o])
+            if e is not None:
+                add_embed(e, 1)
+                store_y(e)
+        store_scales()

@@ -22,9 +22,9 @@ PASSES = T // PASS
 HALF = 512
 PAIR = 256
 
-X_VECTOR = [512, 192, 192, 192, 256, 256, 256, 256]
-STEPS = [(0, None), (1, 0), (2, 1), (3, None), (4, None), (5, 2), (6, 3), (7, 4), (None, 5), (None, 6), (None, 7), (None, None), (None, None)]
-Y_VECTOR = [128, 128, 96, 96, 96, 96, 128, 176]
+X_POOL = [0, 320, 320, 320, 320, 0, 512, 512]
+X_EXTRA_VECTOR = 256
+Y_SHARE = [(0, 0), (256, 0), (160, 0), (256, 0), (0, 0), (0, 128), (0, 96), (0, 176)]
 
 
 def tile_soft_dispatch_expert_inputs_g2_kernel(
@@ -38,84 +38,113 @@ def tile_soft_dispatch_expert_inputs_g2_kernel(
         def tiles(name, count, shape, dtype):
             return [sb.tile(shape, dtype, name="%s%d" % (name, n), align_bytes=64) for n in range(count)]
 
-        banks = [ps.tile([P, 512], F32, name="bank%d" % n) for n in range(8)]
+        banks = [ps.tile([P, 512], F32, name="bank%d" % n) for n in range(7)]
+        weight = ps.tile([P, P, PACK], F32, name="weight")
         ident = sb.tile([P, P], F32, name="ident", align_bytes=64)
-        weight = sb.tile([P, PASSES, PACK], BF16, name="weight", align_bytes=64)
+        weight_raw = sb.tile([PASSES, PASS], BF16, name="weight_raw", align_bytes=64)
+        weight_rows = sb.tile([P, PASS], F32, name="weight_rows", align_bytes=64)
         scale_raw = sb.tile([P, 8, 2], BF16, name="scale_raw", align_bytes=64)
         scale = sb.tile([P, 8], F32, name="scale", align_bytes=64)
-        warm = sb.tile([P, 8], F32, name="warm", align_bytes=64)
         warm_out = sb.tile([P, 8], F32, name="warm_out", align_bytes=64)
+        logit_head = tiles("logit_head", 2, [P, PACK, PAIR], BF16)
+        x_head = tiles("x_head", 2, [P, PACK, PAIR], BF16)
         logit_lo = [None] + tiles("logit_lo", PASSES - 1, [P, PACK, HALF], BF16)
-        logit_hi = sb.tile([P, PASSES, PACK, HALF], BF16, name="logit_hi", align_bytes=64)
+        logit_hi = tiles("logit_hi", 2, [P, PASSES, PACK, PAIR], BF16)
         x_raw = [None] + tiles("x_raw", 2 * PASSES - 1, [P, PACK, HALF], BF16)
-        embed = tiles("embed", 2, [P, PACK, S], BF16)
+        embed = [tiles("embed%d_" % g, 2, [P, PACK, HALF], BF16) for g in range(2)]
         gate = tiles("gate", 2, [P, HALF * PACK], F32)
         disp = tiles("disp", 2, [P, HALF * PACK], BF16)
-        x_words = tiles("x_words", 3, [P, HALF, PACK], BF16)
+        x_words = sb.tile([P, 2 * HALF, PACK], BF16, name="x_words", align_bytes=64)
+        x_extra = sb.tile([P, HALF, PACK], BF16, name="x_extra", align_bytes=64)
         d_codes = tiles("d_codes", 8, [P, HALF], U32)
         d_scales = tiles("d_scales", 8, [P, HALF], U8)
         x_codes = tiles("x_codes", 8, [P, HALF], U32)
         x_scales = tiles("x_scales", 8, [P, HALF], U8)
         scaled = tiles("scaled", 4, [P, PACK, P], F32)
-        y = tiles("y", 3, [P, PACK, PAIR], F32)
-        y_words = tiles("y_words", 2, [P, PAIR, PACK], BF16)
+        y = tiles("y", 4, [P, PACK, PAIR], F32)
+        y_words = tiles("y_words", 3, [P, PAIR, PACK], BF16)
         y_codes = tiles("y_codes", 3, [P, PAIR], U32)
         y_scales = sb.tile([P, 2, S], U8, name="y_scales", align_bytes=64)
-        logit_head = tiles("logit_head", 2, [P, PACK, PAIR], BF16)
-        x_head = tiles("x_head", 2, [P, PACK, PAIR], BF16)
 
         ctx.enter_context(tc.manual_schedule())
 
         def rows(src, k, cols):
             return src[PASS * k : PASS * (k + 1), cols].rearrange("(p j) w -> p j w", j=PACK)
 
-        with nc.allow_non_contiguous_dma(reason="small per-token and per-slot vectors"):
-            nc.scalar.dma_start(out=weight[:], in_=token_weight.rearrange("(k p j) -> p k j", p=P, j=PACK))
-        nc.vector.memset(warm[:], 0.0)
-        nc.scalar.activation(out=warm_out[:], in_=warm[:], func=ACT.Sigmoid)
+        nc.scalar.dma_start(out=weight_raw[:], in_=token_weight.rearrange("(k w) -> k w", k=PASSES))
+        nc.vector.memset(weight_rows[:], 0.0)
+        nc.scalar.activation(out=warm_out[:], in_=weight_rows[:, 0:8], func=ACT.Sigmoid)
         for h in range(2):
             cols = slice(PAIR * h, PAIR * (h + 1))
-            nc.sync.dma_start(out=logit_head[h][:], in_=rows(logits, 0, cols))
             nc.sync.dma_start(out=x_head[h][:], in_=rows(x, 0, cols))
+            nc.sync.dma_start(out=logit_head[h][:], in_=rows(logits, 0, cols))
+
+        def load_x(u):
+            nc.sync.dma_start(out=x_raw[u][:], in_=rows(x, u % 4, slice(HALF * (u // 4), HALF * (u // 4 + 1))))
+
+        def load_hi(n):
+            for k in range(PASSES):
+                nc.sync.dma_start(
+                    out=logit_hi[n][:, k], in_=rows(logits, k, slice(HALF + PAIR * n, HALF + PAIR * (n + 1))))
+
+        def load_embed(g, n):
+            nc.sync.dma_start(out=embed[g][n][:], in_=rows(slot_embed, g, slice(HALF * n, HALF * (n + 1))))
+
         for k in range(1, PASSES):
+            load_x(k)
             nc.sync.dma_start(out=logit_lo[k][:], in_=rows(logits, k, slice(0, HALF)))
-            nc.sync.dma_start(out=x_raw[k][:], in_=rows(x, k, slice(0, HALF)))
-        for k in range(PASSES):
-            nc.sync.dma_start(out=x_raw[PASSES + k][:], in_=rows(x, k, slice(HALF, D)))
-        with nc.allow_non_contiguous_dma(reason="small per-token and per-slot vectors"):
+        load_hi(0)
+        load_x(4)
+        load_x(5)
+        with nc.allow_non_contiguous_dma(reason="one factor to a partition"):
             nc.sync.dma_start(out=scale_raw[:, :, 0:1], in_=slot_scale.rearrange("(i p o) -> p i o", p=P, o=1))
-        nc.sync.dma_start(out=embed[0][:], in_=rows(slot_embed, 0, slice(0, S)))
-        for k in range(PASSES):
-            nc.sync.dma_start(out=logit_hi[:, k], in_=rows(logits, k, slice(HALF, S)))
-        nc.sync.dma_start(out=embed[1][:], in_=rows(slot_embed, 1, slice(0, S)))
+        load_embed(0, 0)
+        load_x(6)
+        load_hi(1)
+        load_x(7)
+        load_embed(1, 0)
+        load_embed(0, 1)
+        load_embed(1, 1)
         make_identity(nc, ident[:])
+        nc.vector.tensor_copy(out=weight_rows[0:PASSES, :], in_=weight_raw[:])
+        for j in range(PACK):
+            nc.tensor.transpose(weight[:, :, j], weight_rows[:, j::PACK], ident[:])
 
-        def interleave(dst, src, width, on_vector):
-            def views(cols):
-                return (
-                    dst[:, cols, :].rearrange("p (c i) t -> p c t i", i=4),
-                    src[:, :, cols].rearrange("p t (c i) -> p c t i", i=4),
-                )
+        def interleave(engine, dst, src):
+            if engine == "pool":
+                nc.gpsimd.tensor_scalar(
+                    out=dst, in0=src.rearrange("p t c -> p c t"),
+                    scalar1=1.0, scalar2=-0.0, op0=ALU.mult, op1=ALU.add)
+                return
+            a = dst.rearrange("p (c i) t -> p c t i", i=4)
+            b = src.rearrange("p t (c i) -> p c t i", i=4)
+            if engine == "vector":
+                nc.vector.tensor_copy(out=a, in_=b)
+            else:
+                nc.scalar.copy(out=a, in_=b)
 
-            def vector_part():
-                if on_vector > 0:
-                    a, b = views(slice(0, on_vector))
-                    nc.vector.tensor_copy(out=a, in_=b)
+        def window(words, width, shared, n):
+            other = width - shared
+            if n % 2 == 0:
+                return words[:, width - other : 2 * width - other, :], slice(other, width), slice(0, other)
+            return words[:, width : 2 * width, :], slice(0, shared), slice(shared, width)
 
-            def scalar_part():
-                if on_vector < width:
-                    a, b = views(slice(on_vector, width))
-                    nc.scalar.copy(out=a, in_=b)
+        def part(engine, words, src, cols):
+            if cols.stop > cols.start:
+                interleave(engine, words[:, cols, :], src[:, :, cols])
 
-            return vector_part, scalar_part
+        def x_pool(u):
+            words, shared, other = window(x_words, HALF, X_POOL[u], u)
+            part("pool", words, x_raw[u], shared)
 
-        def x_parts(u):
-            return interleave(x_words[u % 3], x_raw[u], HALF, X_VECTOR[u])
+        def x_rest(engine, u):
+            words, shared, other = window(x_words, HALF, X_POOL[u], u)
+            part(engine, words, x_raw[u], other)
 
         def x_quantize(u):
+            words = x_extra[:] if u == 5 else window(x_words, HALF, X_POOL[u], u)[0]
             nc.vector.quantize_mx(
-                out=x_codes[u][:].bitcast(FP8X4), scales=x_scales[u][:],
-                in_=x_words[u % 3][:].rearrange("p c t -> p (c t)"))
+                out=x_codes[u][:].bitcast(FP8X4), scales=x_scales[u][:], in_=words.rearrange("p c t -> p (c t)"))
 
         def sigmoid(u):
             if u < PASSES:
@@ -123,10 +152,10 @@ def tile_soft_dispatch_expert_inputs_g2_kernel(
                     out=gate[u % 2][:].rearrange("p (s j) -> p s j", j=PACK),
                     in_=logit_lo[u][:].rearrange("p j s -> p s j"), func=ACT.Sigmoid)
             else:
-                cols = slice(P * (u - 4), P * (u - 3))
+                cols = slice(P * (u % 2), P * (u % 2 + 1))
                 nc.scalar.activation(
                     out=gate[u % 2][:].rearrange("p (k s j) -> p k s j", k=PASSES, j=PACK),
-                    in_=logit_hi[:, :, :, cols].rearrange("p k j s -> p k s j"), func=ACT.Sigmoid)
+                    in_=logit_hi[(u - 4) // 2][:, :, :, cols].rearrange("p k j s -> p k s j"), func=ACT.Sigmoid)
 
         def weigh(u):
             if u < PASSES:
@@ -138,15 +167,15 @@ def tile_soft_dispatch_expert_inputs_g2_kernel(
                 nc.vector.tensor_tensor(
                     out=disp[u % 2][:].rearrange("p (k s j) -> p k s j", k=PASSES, j=PACK),
                     in0=gate[u % 2][:].rearrange("p (k s j) -> p k s j", k=PASSES, j=PACK),
-                    in1=weight[:].unsqueeze(2).to_broadcast([P, PASSES, P, PACK]), op=ALU.mult)
+                    in1=weight[:, 0:PASSES, :].unsqueeze(2).to_broadcast([P, PASSES, P, PACK]), op=ALU.mult)
 
         def d_quantize(u):
             nc.vector.quantize_mx(out=d_codes[u][:].bitcast(FP8X4), scales=d_scales[u][:], in_=disp[u % 2][:])
 
+        bank_number = [[0, 1, 2, 3, 1, 2, 5, 0], [4, 5, 6, 0, 3, 4, 6, 1]]
+
         def bank_of(i, g):
-            if i < 4:
-                return banks[4 * g + i]
-            return banks[4 * ((i - 4) // 2) + 2 * g + i % 2]
+            return banks[bank_number[g][i]]
 
         def mx_pass(i, g, k):
             u, c = (k, i) if i < 4 else (i, k)
@@ -181,23 +210,25 @@ def tile_soft_dispatch_expert_inputs_g2_kernel(
             a, g = units[e]
             i = 2 * a + h
             nc.vector.tensor_tensor(
-                out=y[e % 3][:, :, P * h : P * (h + 1)],
+                out=y[e % 4][:, :, P * h : P * (h + 1)],
                 in0=bank_of(i, g)[:].rearrange("p (t s) -> p t s", t=PACK),
-                in1=embed[g][:, :, P * i : P * (i + 1)], op=ALU.add)
+                in1=embed[g][i // 4][:, :, P * (i % 4) : P * (i % 4 + 1)], op=ALU.add)
 
         def store_y(e):
             a, g = units[e]
-            nc.sync.dma_start(out=rows(out_0, g, slice(PAIR * a, PAIR * (a + 1))), in_=y[e % 3][:])
+            nc.sync.dma_start(out=rows(out_0, g, slice(PAIR * a, PAIR * (a + 1))), in_=y[e % 4][:])
 
-        def y_parts(e):
-            return interleave(y_words[e % 2], y[e % 3], PAIR, Y_VECTOR[e])
+        def y_part(engine, e):
+            pool, vector = Y_SHARE[e]
+            cols = {"pool": slice(0, pool), "vector": slice(pool, pool + vector), "scalar": slice(pool + vector, PAIR)}
+            part(engine, y_words[e % 3][:], y[e % 4], cols[engine])
 
         def y_quantize(e):
             a, g = units[e]
             cols = slice(PAIR * a, PAIR * (a + 1))
             nc.vector.quantize_mx(
                 out=y_codes[e % 3][:].bitcast(FP8X4), scales=y_scales[:, g, cols],
-                in_=y_words[e % 2][:].rearrange("p c t -> p (c t)"))
+                in_=y_words[e % 3][:].rearrange("p c t -> p (c t)"))
             nc.sync.dma_start(
                 out=out_1[g, :, cols, :].rearrange("p m t -> p (m t)").bitcast(I32),
                 in_=y_codes[e % 3][:].bitcast(I32))
@@ -210,82 +241,117 @@ def tile_soft_dispatch_expert_inputs_g2_kernel(
                     in_=y_scales[32 * q : 32 * q + 4, :, :].bitcast(I32))
 
         for h in range(2):
+            interleave("vector", x_words[:, PAIR * h : PAIR * (h + 1), :], x_head[h][:])
             nc.scalar.activation(
                 out=gate[0][:, PAIR * PACK * h : PAIR * PACK * (h + 1)].rearrange("p (s j) -> p s j", j=PACK),
                 in_=logit_head[h][:].rearrange("p j s -> p s j"), func=ACT.Sigmoid)
-            interleave(x_words[0][:, PAIR * h : PAIR * (h + 1), :], x_head[h], PAIR, PAIR)[0]()
-        for k in range(PASSES):
-            if k > 0:
-                xv, xs = x_parts(k)
-                xv()
-                xs()
-                d_quantize(k - 1)
-                for i in range(4):
-                    mx_pass(i, 0, k - 1)
-            weigh(k)
-            if k + 1 < PASSES:
-                sigmoid(k + 1)
-            x_quantize(k)
-        x_parts(4)[1]()
+        x_quantize(0)
+        x_rest("vector", 1)
+
+        def release(e, h):
+            evacuate(e, h)
+            turn(e, h)
+
+        def finish(e):
+            add_embed(e, 0)
+            add_embed(e, 1)
+            store_y(e)
+
+        for n in range(PASSES):
+            x_pool(n + 1)
+            weigh(n)
+            sigmoid(n + 1)
+            x_quantize(n + 1)
+            if n < 3:
+                x_rest("scalar", n + 2)
+            d_quantize(n)
+            for i in range(4):
+                mx_pass(i, 0, n)
         nc.vector.tensor_copy(out=scale[:], in_=scale_raw[:, :, 0])
-        d_quantize(3)
-        for i in range(4):
-            mx_pass(i, 0, 3)
+        part("vector", x_extra[:], x_raw[5], slice(0, X_EXTRA_VECTOR))
+        part("scalar", x_extra[:], x_raw[5], slice(X_EXTRA_VECTOR, HALF))
 
-        operands = [("x", 4), ("x", 5), ("x", 6), ("x", 7), ("d", 4), ("d", 5), ("d", 6), ("d", 7)]
-        steps = STEPS
-
-        def scalar_side(kind, u):
-            if kind == "x":
-                x_parts(u)[1]()
+        for n in range(4, 6):
+            e = n - 4
+            x_pool(n + 2)
+            weigh(n)
+            release(e, 0)
+            release(e, 1)
+            if n == 4:
+                for i in range(3):
+                    mx_pass(i, 1, 0)
             else:
-                sigmoid(u)
-
-        def vector_side(kind, u):
-            if kind == "x":
-                x_parts(u)[0]()
-            else:
-                weigh(u)
-
-        def finish(kind, u):
-            if kind == "x":
-                x_quantize(u)
-            else:
-                d_quantize(u)
-
-        def multiply(kind, u):
-            if kind == "x":
+                mx_pass(3, 1, 0)
+                mx_pass(3, 1, 1)
                 for i in range(4):
-                    mx_pass(i, 1, u - 4)
-            else:
-                mx_group(u, 0)
-                mx_group(u, 1)
+                    mx_pass(i, 1, 2)
+            sigmoid(n + 1)
+            if e > 0:
+                y_part("scalar", e - 1)
+            finish(e)
+            if n == 4:
+                x_quantize(5)
+                for i in range(3):
+                    mx_pass(i, 1, 1)
+            x_quantize(n + 2)
+            if n == 5:
+                for i in range(4):
+                    mx_pass(i, 1, 3)
+            d_quantize(n)
+            mx_group(n, 0)
+            if e > 0:
+                y_quantize(e - 1)
 
-        results = [e for (o, e) in steps]
-        for n, (o, e) in enumerate(steps):
-            words = results[n - 1] if n >= 1 else None
-            codes = results[n - 2] if n >= 2 else None
-            if e is not None:
-                evacuate(e, 0)
-                evacuate(e, 1)
-                turn(e, 0)
-                turn(e, 1)
-            if n > 0 and steps[n - 1][0] is not None:
-                multiply(*operands[steps[n - 1][0]])
-            if o is not None:
-                vector_side(*operands[o])
-                if o + 1 < len(operands):
-                    scalar_side(*operands[o + 1])
-            if codes is not None:
-                y_quantize(codes)
-            if words is not None:
-                y_parts(words)[0]()
-                y_parts(words)[1]()
-            if e is not None:
-                add_embed(e, 0)
-            if o is not None:
-                finish(*operands[o])
-            if e is not None:
-                add_embed(e, 1)
-                store_y(e)
+        y_part("pool", 1)
+        weigh(6)
+        release(2, 0)
+        release(2, 1)
+        release(3, 0)
+        release(3, 1)
+        mx_group(4, 1)
+        sigmoid(7)
+        finish(2)
+        mx_group(5, 1)
+        y_part("pool", 2)
+        y_part("scalar", 2)
+        finish(3)
+        d_quantize(6)
+        y_quantize(1)
+        y_quantize(2)
+
+        y_part("pool", 3)
+        weigh(7)
+        mx_group(6, 0)
+        release(4, 0)
+        release(4, 1)
+        mx_group(6, 1)
+        release(5, 0)
+        release(5, 1)
+        y_quantize(3)
+        d_quantize(7)
+        mx_group(7, 0)
+        release(6, 0)
+        finish(4)
+        release(7, 0)
+        mx_group(7, 1)
+        y_part("scalar", 4)
+        finish(5)
+        release(6, 1)
+        release(7, 1)
+        y_part("vector", 5)
+        y_part("scalar", 5)
+        add_embed(6, 0)
+        y_quantize(4)
+        add_embed(7, 0)
+        add_embed(6, 1)
+        store_y(6)
+        y_part("scalar", 6)
+        add_embed(7, 1)
+        store_y(7)
+        y_quantize(5)
+        y_part("vector", 6)
+        y_part("scalar", 7)
+        y_part("vector", 7)
+        y_quantize(6)
+        y_quantize(7)
         store_scales()

@@ -22,9 +22,11 @@ PASSES = T // PASS
 HALF = 512
 PAIR = 256
 
-X_POOL = [0, 320, 320, 320, 320, 0, 512, 512]
-X_EXTRA_VECTOR = 256
-Y_SHARE = [(0, 0), (256, 0), (160, 0), (256, 0), (0, 0), (0, 128), (0, 96), (0, 176)]
+X_POOL = [0, 288, 288, 288, 288, 0, 288, 512]
+RUN = 2
+LAST_VECTOR = 88
+Y0_POOL = 128
+Y3_POOL = 160
 
 
 def tile_soft_dispatch_expert_inputs_g2_kernel(
@@ -60,10 +62,10 @@ def tile_soft_dispatch_expert_inputs_g2_kernel(
         d_scales = tiles("d_scales", 8, [P, HALF], U8)
         x_codes = tiles("x_codes", 8, [P, HALF], U32)
         x_scales = tiles("x_scales", 8, [P, HALF], U8)
-        scaled = tiles("scaled", 4, [P, PACK, P], F32)
+        scaled = tiles("scaled", 6, [P, PACK, P], F32)
         y = tiles("y", 4, [P, PACK, PAIR], F32)
-        y_words = tiles("y_words", 3, [P, PAIR, PACK], BF16)
-        y_codes = tiles("y_codes", 3, [P, PAIR], U32)
+        y_words = tiles("y_words", 2, [P, 2, PAIR, PACK], BF16)
+        y_codes = tiles("y_codes", 3, [P, 2, PAIR], U32)
         y_scales = sb.tile([P, 2, S], U8, name="y_scales", align_bytes=64)
 
         ctx.enter_context(tc.manual_schedule())
@@ -146,28 +148,26 @@ def tile_soft_dispatch_expert_inputs_g2_kernel(
             nc.vector.quantize_mx(
                 out=x_codes[u][:].bitcast(FP8X4), scales=x_scales[u][:], in_=words.rearrange("p c t -> p (c t)"))
 
+        def gate_from(dst, src):
+            nc.scalar.activation(
+                out=dst.rearrange("p (c j i) -> p c j i", j=PACK, i=RUN),
+                in_=src.rearrange("p j (c i) -> p c j i", i=RUN), func=ACT.Sigmoid)
+
         def sigmoid(u):
             if u < PASSES:
-                nc.scalar.activation(
-                    out=gate[u % 2][:].rearrange("p (s j) -> p s j", j=PACK),
-                    in_=logit_lo[u][:].rearrange("p j s -> p s j"), func=ACT.Sigmoid)
+                gate_from(gate[u % 2][:], logit_lo[u][:])
             else:
                 cols = slice(P * (u % 2), P * (u % 2 + 1))
-                nc.scalar.activation(
-                    out=gate[u % 2][:].rearrange("p (k s j) -> p k s j", k=PASSES, j=PACK),
-                    in_=logit_hi[(u - 4) // 2][:, :, :, cols].rearrange("p k j s -> p k s j"), func=ACT.Sigmoid)
+                for k in range(PASSES):
+                    gate_from(gate[u % 2][:, PASS * k : PASS * (k + 1)], logit_hi[(u - 4) // 2][:, k, :, cols])
 
         def weigh(u):
-            if u < PASSES:
-                nc.vector.tensor_tensor(
-                    out=disp[u % 2][:].rearrange("p (s j) -> p s j", j=PACK),
-                    in0=gate[u % 2][:].rearrange("p (s j) -> p s j", j=PACK),
-                    in1=weight[:, u : u + 1, :].to_broadcast([P, HALF, PACK]), op=ALU.mult)
-            else:
-                nc.vector.tensor_tensor(
-                    out=disp[u % 2][:].rearrange("p (k s j) -> p k s j", k=PASSES, j=PACK),
-                    in0=gate[u % 2][:].rearrange("p (k s j) -> p k s j", k=PASSES, j=PACK),
-                    in1=weight[:, 0:PASSES, :].unsqueeze(2).to_broadcast([P, PASSES, P, PACK]), op=ALU.mult)
+            k = 1 if u < PASSES else PASSES
+            factor = weight[:, u : u + 1, :] if u < PASSES else weight[:, 0:PASSES, :]
+            nc.vector.tensor_tensor(
+                out=disp[u % 2][:],
+                in0=gate[u % 2][:].rearrange("p (c j i) -> p c i j", i=RUN, j=PACK),
+                in1=factor.unsqueeze(2).to_broadcast([P, k, HALF // k, PACK]), op=ALU.mult)
 
         def d_quantize(u):
             nc.vector.quantize_mx(out=d_codes[u][:].bitcast(FP8X4), scales=d_scales[u][:], in_=disp[u % 2][:])
@@ -196,7 +196,7 @@ def tile_soft_dispatch_expert_inputs_g2_kernel(
             a, g = units[e]
             i = 2 * a + h
             nc.scalar.activation(
-                out=scaled[(2 * e + h) % 4][:],
+                out=scaled[(2 * e + h) % 6][:],
                 in_=bank_of(i, g)[:].rearrange("p (m t) -> p t m", t=PACK),
                 func=ACT.Copy, scale=scale[:, i : i + 1])
 
@@ -204,7 +204,7 @@ def tile_soft_dispatch_expert_inputs_g2_kernel(
             a, g = units[e]
             for t in range(PACK):
                 nc.tensor.transpose(
-                    bank_of(2 * a + h, g)[:, P * t : P * (t + 1)], scaled[(2 * e + h) % 4][:, t, :], ident[:])
+                    bank_of(2 * a + h, g)[:, P * t : P * (t + 1)], scaled[(2 * e + h) % 6][:, t, :], ident[:])
 
         def add_embed(e, h):
             a, g = units[e]
@@ -214,39 +214,50 @@ def tile_soft_dispatch_expert_inputs_g2_kernel(
                 in0=bank_of(i, g)[:].rearrange("p (t s) -> p t s", t=PACK),
                 in1=embed[g][i // 4][:, :, P * (i % 4) : P * (i % 4 + 1)], op=ALU.add)
 
-        def store_y(e):
+        def store_y(e, cols=slice(0, PAIR)):
             a, g = units[e]
-            nc.sync.dma_start(out=rows(out_0, g, slice(PAIR * a, PAIR * (a + 1))), in_=y[e % 4][:])
-
-        def y_part(engine, e):
-            pool, vector = Y_SHARE[e]
-            cols = {"pool": slice(0, pool), "vector": slice(pool, pool + vector), "scalar": slice(pool + vector, PAIR)}
-            part(engine, y_words[e % 3][:], y[e % 4], cols[engine])
-
-        def y_quantize(e):
-            a, g = units[e]
-            cols = slice(PAIR * a, PAIR * (a + 1))
-            nc.vector.quantize_mx(
-                out=y_codes[e % 3][:].bitcast(FP8X4), scales=y_scales[:, g, cols],
-                in_=y_words[e % 3][:].rearrange("p c t -> p (c t)"))
             nc.sync.dma_start(
-                out=out_1[g, :, cols, :].rearrange("p m t -> p (m t)").bitcast(I32),
-                in_=y_codes[e % 3][:].bitcast(I32))
+                out=rows(out_0, g, slice(PAIR * a + cols.start, PAIR * a + cols.stop)), in_=y[e % 4][:, :, cols])
 
-        def store_scales():
+        def y_part(engine, e, cols=slice(0, PAIR)):
+            part(engine, y_words[e // 2 % 2][:, e % 2], y[e % 4], cols)
+
+        def y_quantize(e, count):
+            a, g = units[e]
+            u = slice(e % 2, e % 2 + count)
+            nc.vector.quantize_mx(
+                out=y_codes[e // 2 % 3][:, u, :].rearrange("p u m -> p (u m)").bitcast(FP8X4),
+                scales=y_scales[:, g, PAIR * a : PAIR * (a + count)],
+                in_=y_words[e // 2 % 2][:, u].rearrange("p u c t -> p (u c t)"))
+
+        def y_quantize_tile(e, h):
+            a, g = units[e]
+            cols = slice(P * h, P * (h + 1))
+            nc.vector.quantize_mx(
+                out=y_codes[e // 2 % 3][:, e % 2, cols].bitcast(FP8X4),
+                scales=y_scales[:, g, P * (2 * a + h) : P * (2 * a + h + 1)],
+                in_=y_words[e // 2 % 2][:, e % 2, cols].rearrange("p c t -> p (c t)"))
+
+        def store_codes(e, cols=slice(0, PAIR)):
+            a, g = units[e]
+            if units[e + 1][1] == g:
+                dst = out_1[g, :, PAIR * a : PAIR * (a + 2), :].rearrange("p (u m) t -> p u (m t)", u=2)
+            else:
+                dst = out_1[:, :, PAIR * a + cols.start : PAIR * a + cols.stop, :].rearrange("g p m t -> p g (m t)")
+            nc.sync.dma_start(out=dst.bitcast(I32), in_=y_codes[e // 2 % 3][:, :, cols].bitcast(I32))
+
+        def store_scales(n, queues):
+            cols = slice(HALF * n, HALF * (n + 1))
             for q in range(4):
-                queue = nc.sync if q % 2 == 0 else nc.scalar
-                queue.dma_start(
-                    out=out_2[:, 4 * q : 4 * q + 4, :].rearrange("g r s -> r g s").bitcast(I32),
-                    in_=y_scales[32 * q : 32 * q + 4, :, :].bitcast(I32))
+                queues[q % len(queues)].dma_start(
+                    out=out_2[:, 4 * q : 4 * q + 4, cols].rearrange("g r s -> r g s").bitcast(I32),
+                    in_=y_scales[32 * q : 32 * q + 4, :, cols].bitcast(I32))
 
         for h in range(2):
             interleave("vector", x_words[:, PAIR * h : PAIR * (h + 1), :], x_head[h][:])
-            nc.scalar.activation(
-                out=gate[0][:, PAIR * PACK * h : PAIR * PACK * (h + 1)].rearrange("p (s j) -> p s j", j=PACK),
-                in_=logit_head[h][:].rearrange("p j s -> p s j"), func=ACT.Sigmoid)
+            gate_from(gate[0][:, PAIR * PACK * h : PAIR * PACK * (h + 1)], logit_head[h][:])
         x_quantize(0)
-        x_rest("vector", 1)
+        x_rest("scalar", 1)
 
         def release(e, h):
             evacuate(e, h)
@@ -257,6 +268,10 @@ def tile_soft_dispatch_expert_inputs_g2_kernel(
             add_embed(e, 1)
             store_y(e)
 
+        def passes(g, k, tiles_):
+            for i in tiles_:
+                mx_pass(i, g, k)
+
         for n in range(PASSES):
             x_pool(n + 1)
             weigh(n)
@@ -265,93 +280,105 @@ def tile_soft_dispatch_expert_inputs_g2_kernel(
             if n < 3:
                 x_rest("scalar", n + 2)
             d_quantize(n)
-            for i in range(4):
-                mx_pass(i, 0, n)
+            passes(0, n, range(4))
         nc.vector.tensor_copy(out=scale[:], in_=scale_raw[:, :, 0])
-        part("vector", x_extra[:], x_raw[5], slice(0, X_EXTRA_VECTOR))
-        part("scalar", x_extra[:], x_raw[5], slice(X_EXTRA_VECTOR, HALF))
 
-        for n in range(4, 6):
-            e = n - 4
-            x_pool(n + 2)
-            weigh(n)
-            release(e, 0)
-            release(e, 1)
-            if n == 4:
-                for i in range(3):
-                    mx_pass(i, 1, 0)
-            else:
-                mx_pass(3, 1, 0)
-                mx_pass(3, 1, 1)
-                for i in range(4):
-                    mx_pass(i, 1, 2)
-            sigmoid(n + 1)
-            if e > 0:
-                y_part("scalar", e - 1)
-            finish(e)
-            if n == 4:
-                x_quantize(5)
-                for i in range(3):
-                    mx_pass(i, 1, 1)
-            x_quantize(n + 2)
-            if n == 5:
-                for i in range(4):
-                    mx_pass(i, 1, 3)
-            d_quantize(n)
-            mx_group(n, 0)
-            if e > 0:
-                y_quantize(e - 1)
+        x_rest("vector", 6)
+        x_pool(6)
+        weigh(4)
+        passes(1, 0, range(3))
+        part("scalar", x_extra[:], x_raw[5], slice(0, HALF))
+        release(0, 0)
+        release(0, 1)
+        sigmoid(5)
+        x_quantize(5)
+        passes(1, 1, range(3))
+        x_quantize(6)
+        passes(1, 2, range(3))
+        d_quantize(4)
+        x_pool(7)
+        x_rest("scalar", 7)
+        finish(0)
+        for k in range(3):
+            passes(1, k, [3])
 
+        weigh(5)
+        release(1, 0)
+        release(1, 1)
+        mx_group(4, 0)
+        sigmoid(6)
+        y_part("scalar", 0, slice(Y0_POOL, PAIR))
+        x_quantize(7)
+        passes(1, 3, range(4))
+        d_quantize(5)
+        finish(1)
         y_part("pool", 1)
+        y_part("pool", 0, slice(0, Y0_POOL))
+
         weigh(6)
         release(2, 0)
         release(2, 1)
+        mx_group(5, 0)
         release(3, 0)
         release(3, 1)
         mx_group(4, 1)
         sigmoid(7)
-        finish(2)
-        mx_group(5, 1)
-        y_part("pool", 2)
-        y_part("scalar", 2)
-        finish(3)
+        add_embed(2, 0)
         d_quantize(6)
-        y_quantize(1)
-        y_quantize(2)
-
-        y_part("pool", 3)
-        weigh(7)
-        mx_group(6, 0)
+        y_quantize(0, 2)
+        store_codes(0)
+        add_embed(2, 1)
+        store_y(2)
+        mx_group(5, 1)
         release(4, 0)
         release(4, 1)
+        mx_group(6, 0)
+        y_part("pool", 2)
+        finish(3)
         mx_group(6, 1)
+        y_part("pool", 3, slice(0, Y3_POOL))
+
+        first, second = slice(0, P), slice(P, PAIR)
+        weigh(7)
         release(5, 0)
         release(5, 1)
-        y_quantize(3)
+        y_part("scalar", 3, slice(Y3_POOL, PAIR))
+        release(6, 0)
+        evacuate(7, 0)
+        y_quantize(2, 2)
+        store_codes(2)
+        store_scales(0, [nc.sync])
         d_quantize(7)
         mx_group(7, 0)
-        release(6, 0)
+        turn(7, 0)
         finish(4)
-        release(7, 0)
         mx_group(7, 1)
-        y_part("scalar", 4)
+        y_part("pool", 4)
         finish(5)
         release(6, 1)
-        release(7, 1)
-        y_part("vector", 5)
-        y_part("scalar", 5)
         add_embed(6, 0)
-        y_quantize(4)
+        store_y(6, first)
+        y_part("pool", 6, first)
+        y_part("scalar", 5, first)
+        release(7, 1)
+        y_part("scalar", 5, second)
         add_embed(7, 0)
+        store_y(7, first)
         add_embed(6, 1)
-        store_y(6)
-        y_part("scalar", 6)
+        store_y(6, second)
+        y_quantize(4, 1)
+        y_part("vector", 7, first)
         add_embed(7, 1)
-        store_y(7)
-        y_quantize(5)
-        y_part("vector", 6)
-        y_part("scalar", 7)
-        y_part("vector", 7)
-        y_quantize(6)
-        y_quantize(7)
-        store_scales()
+        store_y(7, second)
+        y_part("scalar", 6, second)
+        y_part("scalar", 7, slice(P + LAST_VECTOR, PAIR))
+        y_quantize(5, 1)
+        store_codes(4)
+        y_part("vector", 7, slice(P, P + LAST_VECTOR))
+        y_quantize_tile(6, 0)
+        y_quantize_tile(7, 0)
+        store_codes(6, first)
+        y_quantize_tile(6, 1)
+        y_quantize_tile(7, 1)
+        store_codes(6, second)
+        store_scales(1, [nc.scalar, nc.sync])

@@ -26,7 +26,8 @@ X_POOL = [0, 288, 288, 288, 288, 0, 288, 512]
 RUN = 2
 LAST_VECTOR = 88
 Y0_POOL = 128
-Y3_POOL = 160
+Y3_POOL = 256
+Y4_POOL = 128
 
 
 def tile_soft_dispatch_expert_inputs_g2_kernel(
@@ -44,16 +45,14 @@ def tile_soft_dispatch_expert_inputs_g2_kernel(
         weight = ps.tile([P, P, PACK], F32, name="weight")
         ident = sb.tile([P, P], F32, name="ident", align_bytes=64)
         weight_raw = sb.tile([PASSES, PASS], BF16, name="weight_raw", align_bytes=64)
-        weight_rows = sb.tile([P, PASS], F32, name="weight_rows", align_bytes=64)
-        scale_raw = sb.tile([P, 8, 2], BF16, name="scale_raw", align_bytes=64)
+        weight_rows = sb.tile([P, PASS + P], F32, name="weight_rows", align_bytes=64)
+        scale_raw = sb.tile([8, P], BF16, name="scale_raw", align_bytes=64)
         scale = sb.tile([P, 8], F32, name="scale", align_bytes=64)
         warm_out = sb.tile([P, 8], F32, name="warm_out", align_bytes=64)
-        logit_head = tiles("logit_head", 2, [P, PACK, PAIR], BF16)
-        x_head = tiles("x_head", 2, [P, PACK, PAIR], BF16)
-        logit_lo = [None] + tiles("logit_lo", PASSES - 1, [P, PACK, HALF], BF16)
+        logit_lo = tiles("logit_lo", PASSES, [P, PACK, HALF], BF16)
         logit_hi = tiles("logit_hi", 2, [P, PASSES, PACK, PAIR], BF16)
-        x_raw = [None] + tiles("x_raw", 2 * PASSES - 1, [P, PACK, HALF], BF16)
-        embed = [tiles("embed%d_" % g, 2, [P, PACK, HALF], BF16) for g in range(2)]
+        x_raw = tiles("x_raw", 2 * PASSES, [P, PACK, HALF], BF16)
+        embed = tiles("embed", 2, [P, PACK, S], BF16)
         gate = tiles("gate", 2, [P, HALF * PACK], F32)
         disp = tiles("disp", 2, [P, HALF * PACK], BF16)
         x_words = sb.tile([P, 2 * HALF, PACK], BF16, name="x_words", align_bytes=64)
@@ -63,7 +62,7 @@ def tile_soft_dispatch_expert_inputs_g2_kernel(
         x_codes = tiles("x_codes", 8, [P, HALF], U32)
         x_scales = tiles("x_scales", 8, [P, HALF], U8)
         scaled = tiles("scaled", 6, [P, PACK, P], F32)
-        y = tiles("y", 4, [P, PACK, PAIR], F32)
+        y = tiles("y", 2, [P, PACK, 2 * PAIR], F32)
         y_words = tiles("y_words", 2, [P, 2, PAIR, PACK], BF16)
         y_codes = tiles("y_codes", 3, [P, 2, PAIR], U32)
         y_scales = sb.tile([P, 2, S], U8, name="y_scales", align_bytes=64)
@@ -74,12 +73,9 @@ def tile_soft_dispatch_expert_inputs_g2_kernel(
             return src[PASS * k : PASS * (k + 1), cols].rearrange("(p j) w -> p j w", j=PACK)
 
         nc.scalar.dma_start(out=weight_raw[:], in_=token_weight.rearrange("(k w) -> k w", k=PASSES))
+        nc.scalar.dma_start(out=scale_raw[:], in_=slot_scale.rearrange("(i p) -> i p", p=P))
         nc.vector.memset(weight_rows[:], 0.0)
         nc.scalar.activation(out=warm_out[:], in_=weight_rows[:, 0:8], func=ACT.Sigmoid)
-        for h in range(2):
-            cols = slice(PAIR * h, PAIR * (h + 1))
-            nc.sync.dma_start(out=x_head[h][:], in_=rows(x, 0, cols))
-            nc.sync.dma_start(out=logit_head[h][:], in_=rows(logits, 0, cols))
 
         def load_x(u):
             nc.sync.dma_start(out=x_raw[u][:], in_=rows(x, u % 4, slice(HALF * (u // 4), HALF * (u // 4 + 1))))
@@ -89,28 +85,32 @@ def tile_soft_dispatch_expert_inputs_g2_kernel(
                 nc.sync.dma_start(
                     out=logit_hi[n][:, k], in_=rows(logits, k, slice(HALF + PAIR * n, HALF + PAIR * (n + 1))))
 
-        def load_embed(g, n):
-            nc.sync.dma_start(out=embed[g][n][:], in_=rows(slot_embed, g, slice(HALF * n, HALF * (n + 1))))
+        def load_embed(g, cols):
+            nc.sync.dma_start(out=embed[g][:, :, cols], in_=rows(slot_embed, g, cols))
 
+        def load_lo(k):
+            nc.sync.dma_start(out=logit_lo[k][:], in_=rows(logits, k, slice(0, HALF)))
+
+        load_lo(0)
+        load_x(0)
         for k in range(1, PASSES):
             load_x(k)
-            nc.sync.dma_start(out=logit_lo[k][:], in_=rows(logits, k, slice(0, HALF)))
-        load_hi(0)
+            load_lo(k)
         load_x(4)
+        load_hi(0)
         load_x(5)
-        with nc.allow_non_contiguous_dma(reason="one factor to a partition"):
-            nc.sync.dma_start(out=scale_raw[:, :, 0:1], in_=slot_scale.rearrange("(i p o) -> p i o", p=P, o=1))
-        load_embed(0, 0)
         load_x(6)
-        load_hi(1)
+        load_embed(0, slice(0, HALF))
         load_x(7)
-        load_embed(1, 0)
-        load_embed(0, 1)
-        load_embed(1, 1)
+        load_hi(1)
+        load_embed(1, slice(0, S))
+        load_embed(0, slice(HALF, S))
         make_identity(nc, ident[:])
-        nc.vector.tensor_copy(out=weight_rows[0:PASSES, :], in_=weight_raw[:])
+        nc.vector.tensor_copy(out=weight_rows[0:PASSES, 0:PASS], in_=weight_raw[:])
+        nc.vector.tensor_copy(out=weight_rows[0:8, PASS:], in_=scale_raw[:])
         for j in range(PACK):
-            nc.tensor.transpose(weight[:, :, j], weight_rows[:, j::PACK], ident[:])
+            nc.tensor.transpose(weight[:, :, j], weight_rows[:, j:PASS:PACK], ident[:])
+        nc.tensor.transpose(banks[6][:, 0:P], weight_rows[:, PASS:], ident[:])
 
         def interleave(engine, dst, src):
             if engine == "pool":
@@ -192,6 +192,9 @@ def tile_soft_dispatch_expert_inputs_g2_kernel(
 
         units = [(0, 0), (1, 0), (0, 1), (1, 1), (2, 0), (2, 1), (3, 0), (3, 1)]
 
+        def y_of(e):
+            return y[e // 2 % 2][:, :, PAIR * (e % 2) : PAIR * (e % 2 + 1)]
+
         def evacuate(e, h):
             a, g = units[e]
             i = 2 * a + h
@@ -210,17 +213,17 @@ def tile_soft_dispatch_expert_inputs_g2_kernel(
             a, g = units[e]
             i = 2 * a + h
             nc.vector.tensor_tensor(
-                out=y[e % 4][:, :, P * h : P * (h + 1)],
+                out=y_of(e)[:, :, P * h : P * (h + 1)],
                 in0=bank_of(i, g)[:].rearrange("p (t s) -> p t s", t=PACK),
-                in1=embed[g][i // 4][:, :, P * (i % 4) : P * (i % 4 + 1)], op=ALU.add)
+                in1=embed[g][:, :, P * i : P * (i + 1)], op=ALU.add)
 
         def store_y(e, cols=slice(0, PAIR)):
             a, g = units[e]
             nc.sync.dma_start(
-                out=rows(out_0, g, slice(PAIR * a + cols.start, PAIR * a + cols.stop)), in_=y[e % 4][:, :, cols])
+                out=rows(out_0, g, slice(PAIR * a + cols.start, PAIR * a + cols.stop)), in_=y_of(e)[:, :, cols])
 
         def y_part(engine, e, cols=slice(0, PAIR)):
-            part(engine, y_words[e // 2 % 2][:, e % 2], y[e % 4], cols)
+            part(engine, y_words[e // 2 % 2][:, e % 2], y_of(e), cols)
 
         def y_quantize(e, count):
             a, g = units[e]
@@ -253,10 +256,9 @@ def tile_soft_dispatch_expert_inputs_g2_kernel(
                     out=out_2[:, 4 * q : 4 * q + 4, cols].rearrange("g r s -> r g s").bitcast(I32),
                     in_=y_scales[32 * q : 32 * q + 4, :, cols].bitcast(I32))
 
-        for h in range(2):
-            interleave("vector", x_words[:, PAIR * h : PAIR * (h + 1), :], x_head[h][:])
-            gate_from(gate[0][:, PAIR * PACK * h : PAIR * PACK * (h + 1)], logit_head[h][:])
-        x_quantize(0)
+        sigmoid(0)
+        x_rest("vector", 0)
+        nc.scalar.copy(out=scale[:], in_=banks[6][:, 0:8])
         x_rest("scalar", 1)
 
         def release(e, h):
@@ -276,12 +278,13 @@ def tile_soft_dispatch_expert_inputs_g2_kernel(
             x_pool(n + 1)
             weigh(n)
             sigmoid(n + 1)
+            if n == 0:
+                x_quantize(0)
             x_quantize(n + 1)
             if n < 3:
                 x_rest("scalar", n + 2)
             d_quantize(n)
             passes(0, n, range(4))
-        nc.vector.tensor_copy(out=scale[:], in_=scale_raw[:, :, 0])
 
         x_rest("vector", 6)
         x_pool(6)
@@ -329,55 +332,54 @@ def tile_soft_dispatch_expert_inputs_g2_kernel(
         store_codes(0)
         add_embed(2, 1)
         store_y(2)
-        mx_group(5, 1)
         release(4, 0)
         release(4, 1)
+        mx_group(5, 1)
         mx_group(6, 0)
         y_part("pool", 2)
         finish(3)
         mx_group(6, 1)
         y_part("pool", 3, slice(0, Y3_POOL))
+        finish(4)
 
         first, second = slice(0, P), slice(P, PAIR)
+        y_part("pool", 4, slice(0, Y4_POOL))
         weigh(7)
         release(5, 0)
         release(5, 1)
         y_part("scalar", 3, slice(Y3_POOL, PAIR))
         release(6, 0)
-        evacuate(7, 0)
+        y_part("scalar", 4, slice(Y4_POOL, PAIR))
+        release(7, 0)
         y_quantize(2, 2)
         store_codes(2)
         store_scales(0, [nc.sync])
         d_quantize(7)
         mx_group(7, 0)
-        turn(7, 0)
-        finish(4)
         mx_group(7, 1)
-        y_part("pool", 4)
         finish(5)
-        release(6, 1)
-        add_embed(6, 0)
-        store_y(6, first)
-        y_part("pool", 6, first)
-        y_part("scalar", 5, first)
-        release(7, 1)
+        y_part("pool", 5, first)
         y_part("scalar", 5, second)
-        add_embed(7, 0)
-        store_y(7, first)
-        add_embed(6, 1)
-        store_y(6, second)
+        for e in (6, 7):
+            add_embed(e, 0)
+            store_y(e, first)
+        release(6, 1)
+        release(7, 1)
         y_quantize(4, 1)
-        y_part("vector", 7, first)
-        add_embed(7, 1)
-        store_y(7, second)
-        y_part("scalar", 6, second)
-        y_part("scalar", 7, slice(P + LAST_VECTOR, PAIR))
         y_quantize(5, 1)
         store_codes(4)
-        y_part("vector", 7, slice(P, P + LAST_VECTOR))
+        y_part("vector", 6, first)
+        y_part("vector", 7, first)
         y_quantize_tile(6, 0)
+        add_embed(6, 1)
+        store_y(6, second)
+        y_part("scalar", 6, second)
         y_quantize_tile(7, 0)
         store_codes(6, first)
+        add_embed(7, 1)
+        store_y(7, second)
+        y_part("scalar", 7, slice(P + LAST_VECTOR, PAIR))
+        y_part("vector", 7, slice(P, P + LAST_VECTOR))
         y_quantize_tile(6, 1)
         y_quantize_tile(7, 1)
         store_codes(6, second)

@@ -20,14 +20,19 @@ PACK = 4
 PASS = P * PACK
 PASSES = T // PASS
 HALF = 512
-PAIR = 256
+PAIR = 2 * P
+TILES = S // P
+EARLY_TILES = HALF // P
+RUN = 4
 
-X_POOL = [0, 288, 288, 288, 288, 0, 288, 512]
-RUN = 2
-LAST_VECTOR = 88
-Y0_POOL = 128
-Y3_POOL = 256
-Y4_POOL = 128
+SHORT_SHARE = 320
+SCALAR_PIECE = 5
+X_POOL = [0, SHORT_SHARE, SHORT_SHARE, SHORT_SHARE, SHORT_SHARE, 0, SHORT_SHARE, HALF]
+FIRST_RESULT_POOL = 96
+
+RESULTS = [(0, 0), (1, 0), (0, 1), (1, 1), (2, 0), (2, 1), (3, 0), (3, 1)]
+BANK = [[0, 1, 2, 3, 1, 2, 5, 0], [4, 5, 6, 0, 3, 4, 6, 1]]
+SCALED_BUFS = 6
 
 
 def tile_soft_dispatch_expert_inputs_g2_kernel(
@@ -41,27 +46,26 @@ def tile_soft_dispatch_expert_inputs_g2_kernel(
         def tiles(name, count, shape, dtype):
             return [sb.tile(shape, dtype, name="%s%d" % (name, n), align_bytes=64) for n in range(count)]
 
-        banks = [ps.tile([P, 512], F32, name="bank%d" % n) for n in range(7)]
+        banks = [ps.tile([P, HALF], F32, name="bank%d" % n) for n in range(7)]
         weight = ps.tile([P, P, PACK], F32, name="weight")
         ident = sb.tile([P, P], F32, name="ident", align_bytes=64)
         weight_raw = sb.tile([PASSES, PASS], BF16, name="weight_raw", align_bytes=64)
-        weight_rows = sb.tile([P, PASS + P], F32, name="weight_rows", align_bytes=64)
-        scale_raw = sb.tile([8, P], BF16, name="scale_raw", align_bytes=64)
-        scale = sb.tile([P, 8], F32, name="scale", align_bytes=64)
-        warm_out = sb.tile([P, 8], F32, name="warm_out", align_bytes=64)
-        logit_lo = tiles("logit_lo", PASSES, [P, PACK, HALF], BF16)
-        logit_hi = tiles("logit_hi", 2, [P, PASSES, PACK, PAIR], BF16)
+        factor_rows = sb.tile([P, PASS + P], F32, name="factor_rows", align_bytes=64)
+        scale_raw = sb.tile([TILES, P], BF16, name="scale_raw", align_bytes=64)
+        scale = sb.tile([P, TILES], F32, name="scale", align_bytes=64)
+        logit_early = tiles("logit_early", PASSES, [P, PACK, HALF], BF16)
+        logit_late = tiles("logit_late", 2, [P, PASSES, PACK, PAIR], BF16)
         x_raw = tiles("x_raw", 2 * PASSES, [P, PACK, HALF], BF16)
         embed = tiles("embed", 2, [P, PACK, S], BF16)
         gate = tiles("gate", 2, [P, HALF * PACK], F32)
-        disp = tiles("disp", 2, [P, HALF * PACK], BF16)
+        dispatch = tiles("dispatch", 2, [P, HALF * PACK], BF16)
         x_words = sb.tile([P, 2 * HALF, PACK], BF16, name="x_words", align_bytes=64)
-        x_extra = sb.tile([P, HALF, PACK], BF16, name="x_extra", align_bytes=64)
-        d_codes = tiles("d_codes", 8, [P, HALF], U32)
-        d_scales = tiles("d_scales", 8, [P, HALF], U8)
-        x_codes = tiles("x_codes", 8, [P, HALF], U32)
-        x_scales = tiles("x_scales", 8, [P, HALF], U8)
-        scaled = tiles("scaled", 6, [P, PACK, P], F32)
+        x_words_scalar = sb.tile([P, HALF, PACK], BF16, name="x_words_scalar", align_bytes=64)
+        d_codes = tiles("d_codes", TILES, [P, HALF], U32)
+        d_scales = tiles("d_scales", TILES, [P, HALF], U8)
+        x_codes = tiles("x_codes", 2 * PASSES, [P, HALF], U32)
+        x_scales = tiles("x_scales", 2 * PASSES, [P, HALF], U8)
+        scaled = tiles("scaled", SCALED_BUFS, [P, PACK, P], F32)
         y = tiles("y", 2, [P, PACK, 2 * PAIR], F32)
         y_words = tiles("y_words", 2, [P, 2, PAIR, PACK], BF16)
         y_codes = tiles("y_codes", 3, [P, 2, PAIR], U32)
@@ -70,171 +74,164 @@ def tile_soft_dispatch_expert_inputs_g2_kernel(
         ctx.enter_context(tc.manual_schedule())
 
         def rows(src, k, cols):
-            return src[PASS * k : PASS * (k + 1), cols].rearrange("(p j) w -> p j w", j=PACK)
+            return src[PASS * k : PASS * (k + 1), cols].rearrange("(p t) w -> p t w", t=PACK)
 
         nc.scalar.dma_start(out=weight_raw[:], in_=token_weight.rearrange("(k w) -> k w", k=PASSES))
         nc.scalar.dma_start(out=scale_raw[:], in_=slot_scale.rearrange("(i p) -> i p", p=P))
-        nc.vector.memset(weight_rows[:], 0.0)
-        nc.scalar.activation(out=warm_out[:], in_=weight_rows[:, 0:8], func=ACT.Sigmoid)
+        nc.vector.memset(factor_rows[:], 0.0)
 
         def load_x(u):
-            nc.sync.dma_start(out=x_raw[u][:], in_=rows(x, u % 4, slice(HALF * (u // 4), HALF * (u // 4 + 1))))
+            group = u // PASSES
+            nc.sync.dma_start(out=x_raw[u][:], in_=rows(x, u % PASSES, slice(HALF * group, HALF * (group + 1))))
 
-        def load_hi(n):
+        def load_early(k):
+            nc.sync.dma_start(out=logit_early[k][:], in_=rows(logits, k, slice(0, HALF)))
+
+        def load_late(n):
             for k in range(PASSES):
                 nc.sync.dma_start(
-                    out=logit_hi[n][:, k], in_=rows(logits, k, slice(HALF + PAIR * n, HALF + PAIR * (n + 1))))
+                    out=logit_late[n][:, k], in_=rows(logits, k, slice(HALF + PAIR * n, HALF + PAIR * (n + 1))))
 
         def load_embed(g, cols):
             nc.sync.dma_start(out=embed[g][:, :, cols], in_=rows(slot_embed, g, cols))
 
-        def load_lo(k):
-            nc.sync.dma_start(out=logit_lo[k][:], in_=rows(logits, k, slice(0, HALF)))
-
-        load_lo(0)
+        load_early(0)
         load_x(0)
         for k in range(1, PASSES):
             load_x(k)
-            load_lo(k)
+            load_early(k)
         load_x(4)
-        load_hi(0)
+        load_late(0)
         load_x(5)
         load_x(6)
         load_embed(0, slice(0, HALF))
         load_x(7)
-        load_hi(1)
+        load_late(1)
         load_embed(1, slice(0, S))
         load_embed(0, slice(HALF, S))
-        make_identity(nc, ident[:])
-        nc.vector.tensor_copy(out=weight_rows[0:PASSES, 0:PASS], in_=weight_raw[:])
-        nc.vector.tensor_copy(out=weight_rows[0:8, PASS:], in_=scale_raw[:])
-        for j in range(PACK):
-            nc.tensor.transpose(weight[:, :, j], weight_rows[:, j:PASS:PACK], ident[:])
-        nc.tensor.transpose(banks[6][:, 0:P], weight_rows[:, PASS:], ident[:])
 
-        def interleave(engine, dst, src):
+        make_identity(nc, ident[:])
+        nc.vector.tensor_copy(out=factor_rows[0:PASSES, 0:PASS], in_=weight_raw[:])
+        nc.vector.tensor_copy(out=factor_rows[0:TILES, PASS:], in_=scale_raw[:])
+        for t in range(PACK):
+            nc.tensor.transpose(weight[:, :, t], factor_rows[:, t:PASS:PACK], ident[:])
+        nc.tensor.transpose(banks[6][:, 0:P], factor_rows[:, PASS:], ident[:])
+
+        def interleave(engine, words, src, cols):
+            dst, src = words[:, cols, :], src[:, :, cols]
             if engine == "pool":
                 nc.gpsimd.tensor_scalar(
                     out=dst, in0=src.rearrange("p t c -> p c t"),
                     scalar1=1.0, scalar2=-0.0, op0=ALU.mult, op1=ALU.add)
                 return
-            a = dst.rearrange("p (c i) t -> p c t i", i=4)
-            b = src.rearrange("p t (c i) -> p c t i", i=4)
+            dst = dst.rearrange("p (c i) t -> p c t i", i=RUN)
+            src = src.rearrange("p t (c i) -> p c t i", i=RUN)
             if engine == "vector":
-                nc.vector.tensor_copy(out=a, in_=b)
+                nc.vector.tensor_copy(out=dst, in_=src)
             else:
-                nc.scalar.copy(out=a, in_=b)
+                nc.scalar.copy(out=dst, in_=src)
 
-        def window(words, width, shared, n):
-            other = width - shared
-            if n % 2 == 0:
-                return words[:, width - other : 2 * width - other, :], slice(other, width), slice(0, other)
-            return words[:, width : 2 * width, :], slice(0, shared), slice(shared, width)
-
-        def part(engine, words, src, cols):
-            if cols.stop > cols.start:
-                interleave(engine, words[:, cols, :], src[:, :, cols])
+        def x_window(u):
+            rest = HALF - X_POOL[u]
+            if u % 2 == 0:
+                return x_words[:, HALF - rest : 2 * HALF - rest, :], slice(rest, HALF), slice(0, rest)
+            return x_words[:, HALF:, :], slice(0, X_POOL[u]), slice(X_POOL[u], HALF)
 
         def x_pool(u):
-            words, shared, other = window(x_words, HALF, X_POOL[u], u)
-            part("pool", words, x_raw[u], shared)
+            words, pool_cols, rest_cols = x_window(u)
+            interleave("pool", words, x_raw[u], pool_cols)
 
         def x_rest(engine, u):
-            words, shared, other = window(x_words, HALF, X_POOL[u], u)
-            part(engine, words, x_raw[u], other)
+            words, pool_cols, rest_cols = x_window(u)
+            interleave(engine, words, x_raw[u], rest_cols)
 
         def x_quantize(u):
-            words = x_extra[:] if u == 5 else window(x_words, HALF, X_POOL[u], u)[0]
+            words = x_words_scalar[:] if u == SCALAR_PIECE else x_window(u)[0]
             nc.vector.quantize_mx(
                 out=x_codes[u][:].bitcast(FP8X4), scales=x_scales[u][:], in_=words.rearrange("p c t -> p (c t)"))
 
-        def gate_from(dst, src):
-            nc.scalar.activation(
-                out=dst.rearrange("p (c j i) -> p c j i", j=PACK, i=RUN),
-                in_=src.rearrange("p j (c i) -> p c j i", i=RUN), func=ACT.Sigmoid)
-
-        def sigmoid(u):
-            if u < PASSES:
-                gate_from(gate[u % 2][:], logit_lo[u][:])
+        def sigmoid(n):
+            if n < EARLY_TILES:
+                dst = gate[n % 2][:].rearrange("p (s t) -> p s t", t=PACK)
+                src = logit_early[n][:].rearrange("p t s -> p s t")
             else:
-                cols = slice(P * (u % 2), P * (u % 2 + 1))
-                for k in range(PASSES):
-                    gate_from(gate[u % 2][:, PASS * k : PASS * (k + 1)], logit_hi[(u - 4) // 2][:, k, :, cols])
+                cols = slice(P * (n % 2), P * (n % 2 + 1))
+                dst = gate[n % 2][:].rearrange("p (k s t) -> p k s t", k=PASSES, t=PACK)
+                src = logit_late[(n - EARLY_TILES) // 2][:, :, :, cols].rearrange("p k t s -> p k s t")
+            nc.scalar.activation(out=dst, in_=src, func=ACT.Sigmoid)
 
-        def weigh(u):
-            k = 1 if u < PASSES else PASSES
-            factor = weight[:, u : u + 1, :] if u < PASSES else weight[:, 0:PASSES, :]
+        def weigh(n):
+            count = 1 if n < EARLY_TILES else PASSES
+            factor = weight[:, n : n + 1, :] if n < EARLY_TILES else weight[:, 0:PASSES, :]
             nc.vector.tensor_tensor(
-                out=disp[u % 2][:],
-                in0=gate[u % 2][:].rearrange("p (c j i) -> p c i j", i=RUN, j=PACK),
-                in1=factor.unsqueeze(2).to_broadcast([P, k, HALF // k, PACK]), op=ALU.mult)
+                out=dispatch[n % 2][:].rearrange("p (k s t) -> p k s t", k=count, t=PACK),
+                in0=gate[n % 2][:].rearrange("p (k s t) -> p k s t", k=count, t=PACK),
+                in1=factor.unsqueeze(2).to_broadcast([P, count, HALF // count, PACK]), op=ALU.mult)
 
-        def d_quantize(u):
-            nc.vector.quantize_mx(out=d_codes[u][:].bitcast(FP8X4), scales=d_scales[u][:], in_=disp[u % 2][:])
-
-        bank_number = [[0, 1, 2, 3, 1, 2, 5, 0], [4, 5, 6, 0, 3, 4, 6, 1]]
-
-        def bank_of(i, g):
-            return banks[bank_number[g][i]]
+        def d_quantize(n):
+            nc.vector.quantize_mx(out=d_codes[n][:].bitcast(FP8X4), scales=d_scales[n][:], in_=dispatch[n % 2][:])
 
         def mx_pass(i, g, k):
-            u, c = (k, i) if i < 4 else (i, k)
-            cols = slice(P * c, P * (c + 1))
+            n, block = (k, i) if i < EARLY_TILES else (i, k)
+            cols = slice(P * block, P * (block + 1))
             nc.tensor.matmul_mx(
-                out=bank_of(i, g)[:],
-                lhsT=d_codes[u][:, cols].bitcast(FP8X4), lhsT_scale=d_scales[u][:, cols],
+                out=banks[BANK[g][i]][:],
+                lhsT=d_codes[n][:, cols].bitcast(FP8X4), lhsT_scale=d_scales[n][:, cols],
                 rhs=x_codes[PASSES * g + k][:].bitcast(FP8X4), rhs_scale=x_scales[PASSES * g + k][:],
                 start=(k == 0), stop=(k == PASSES - 1))
+
+        def pass_over(slot_tiles, g, k):
+            for i in slot_tiles:
+                mx_pass(i, g, k)
 
         def mx_group(i, g):
             for k in range(PASSES):
                 mx_pass(i, g, k)
 
-        units = [(0, 0), (1, 0), (0, 1), (1, 1), (2, 0), (2, 1), (3, 0), (3, 1)]
-
         def y_of(e):
             return y[e // 2 % 2][:, :, PAIR * (e % 2) : PAIR * (e % 2 + 1)]
 
-        def evacuate(e, h):
-            a, g = units[e]
+        def release(e, h):
+            a, g = RESULTS[e]
             i = 2 * a + h
+            bank, rows_t = banks[BANK[g][i]], scaled[(2 * e + h) % SCALED_BUFS]
             nc.scalar.activation(
-                out=scaled[(2 * e + h) % 6][:],
-                in_=bank_of(i, g)[:].rearrange("p (m t) -> p t m", t=PACK),
+                out=rows_t[:], in_=bank[:].rearrange("p (m t) -> p t m", t=PACK),
                 func=ACT.Copy, scale=scale[:, i : i + 1])
-
-        def turn(e, h):
-            a, g = units[e]
             for t in range(PACK):
-                nc.tensor.transpose(
-                    bank_of(2 * a + h, g)[:, P * t : P * (t + 1)], scaled[(2 * e + h) % 6][:, t, :], ident[:])
+                nc.tensor.transpose(bank[:, P * t : P * (t + 1)], rows_t[:, t, :], ident[:])
 
         def add_embed(e, h):
-            a, g = units[e]
+            a, g = RESULTS[e]
             i = 2 * a + h
             nc.vector.tensor_tensor(
                 out=y_of(e)[:, :, P * h : P * (h + 1)],
-                in0=bank_of(i, g)[:].rearrange("p (t s) -> p t s", t=PACK),
+                in0=banks[BANK[g][i]][:].rearrange("p (t s) -> p t s", t=PACK),
                 in1=embed[g][:, :, P * i : P * (i + 1)], op=ALU.add)
 
         def store_y(e, cols=slice(0, PAIR)):
-            a, g = units[e]
+            a, g = RESULTS[e]
             nc.sync.dma_start(
                 out=rows(out_0, g, slice(PAIR * a + cols.start, PAIR * a + cols.stop)), in_=y_of(e)[:, :, cols])
 
-        def y_part(engine, e, cols=slice(0, PAIR)):
-            part(engine, y_words[e // 2 % 2][:, e % 2], y_of(e), cols)
+        def finish(e):
+            add_embed(e, 0)
+            add_embed(e, 1)
+            store_y(e)
+
+        def y_interleave(engine, e, cols=slice(0, PAIR)):
+            interleave(engine, y_words[e // 2 % 2][:, e % 2], y_of(e), cols)
 
         def y_quantize(e, count):
-            a, g = units[e]
-            u = slice(e % 2, e % 2 + count)
+            a, g = RESULTS[e]
+            held = slice(e % 2, e % 2 + count)
             nc.vector.quantize_mx(
-                out=y_codes[e // 2 % 3][:, u, :].rearrange("p u m -> p (u m)").bitcast(FP8X4),
+                out=y_codes[e // 2 % 3][:, held, :].rearrange("p u m -> p (u m)").bitcast(FP8X4),
                 scales=y_scales[:, g, PAIR * a : PAIR * (a + count)],
-                in_=y_words[e // 2 % 2][:, u].rearrange("p u c t -> p (u c t)"))
+                in_=y_words[e // 2 % 2][:, held].rearrange("p u c t -> p (u c t)"))
 
         def y_quantize_tile(e, h):
-            a, g = units[e]
+            a, g = RESULTS[e]
             cols = slice(P * h, P * (h + 1))
             nc.vector.quantize_mx(
                 out=y_codes[e // 2 % 3][:, e % 2, cols].bitcast(FP8X4),
@@ -242,15 +239,15 @@ def tile_soft_dispatch_expert_inputs_g2_kernel(
                 in_=y_words[e // 2 % 2][:, e % 2, cols].rearrange("p c t -> p (c t)"))
 
         def store_codes(e, cols=slice(0, PAIR)):
-            a, g = units[e]
-            if units[e + 1][1] == g:
+            a, g = RESULTS[e]
+            if RESULTS[e + 1][1] == g:
                 dst = out_1[g, :, PAIR * a : PAIR * (a + 2), :].rearrange("p (u m) t -> p u (m t)", u=2)
             else:
                 dst = out_1[:, :, PAIR * a + cols.start : PAIR * a + cols.stop, :].rearrange("g p m t -> p g (m t)")
             nc.sync.dma_start(out=dst.bitcast(I32), in_=y_codes[e // 2 % 3][:, :, cols].bitcast(I32))
 
-        def store_scales(n, queues):
-            cols = slice(HALF * n, HALF * (n + 1))
+        def store_scales(half, queues):
+            cols = slice(HALF * half, HALF * (half + 1))
             for q in range(4):
                 queues[q % len(queues)].dma_start(
                     out=out_2[:, 4 * q : 4 * q + 4, cols].rearrange("g r s -> r g s").bitcast(I32),
@@ -258,21 +255,8 @@ def tile_soft_dispatch_expert_inputs_g2_kernel(
 
         sigmoid(0)
         x_rest("vector", 0)
-        nc.scalar.copy(out=scale[:], in_=banks[6][:, 0:8])
+        nc.scalar.copy(out=scale[:], in_=banks[6][:, 0:TILES])
         x_rest("scalar", 1)
-
-        def release(e, h):
-            evacuate(e, h)
-            turn(e, h)
-
-        def finish(e):
-            add_embed(e, 0)
-            add_embed(e, 1)
-            store_y(e)
-
-        def passes(g, k, tiles_):
-            for i in tiles_:
-                mx_pass(i, g, k)
 
         for n in range(PASSES):
             x_pool(n + 1)
@@ -281,49 +265,47 @@ def tile_soft_dispatch_expert_inputs_g2_kernel(
             if n == 0:
                 x_quantize(0)
             x_quantize(n + 1)
-            if n < 3:
+            if n + 1 < PASSES:
                 x_rest("scalar", n + 2)
             d_quantize(n)
-            passes(0, n, range(4))
+            pass_over(range(EARLY_TILES), 0, n)
+
 
         x_rest("vector", 6)
         x_pool(6)
         weigh(4)
-        passes(1, 0, range(3))
-        part("scalar", x_extra[:], x_raw[5], slice(0, HALF))
+        pass_over(range(3), 1, 0)
+        interleave("scalar", x_words_scalar[:], x_raw[SCALAR_PIECE], slice(0, HALF))
         release(0, 0)
         release(0, 1)
         sigmoid(5)
         x_quantize(5)
-        passes(1, 1, range(3))
+        pass_over(range(3), 1, 1)
         x_quantize(6)
-        passes(1, 2, range(3))
+        pass_over(range(3), 1, 2)
         d_quantize(4)
         x_pool(7)
-        x_rest("scalar", 7)
         finish(0)
         for k in range(3):
-            passes(1, k, [3])
+            mx_pass(3, 1, k)
 
         weigh(5)
         release(1, 0)
         release(1, 1)
         mx_group(4, 0)
         sigmoid(6)
-        y_part("scalar", 0, slice(Y0_POOL, PAIR))
+        y_interleave("scalar", 0, slice(FIRST_RESULT_POOL, PAIR))
         x_quantize(7)
-        passes(1, 3, range(4))
+        pass_over(range(EARLY_TILES), 1, 3)
         d_quantize(5)
         finish(1)
-        y_part("pool", 1)
-        y_part("pool", 0, slice(0, Y0_POOL))
+        y_interleave("pool", 1)
+        y_interleave("pool", 0, slice(0, FIRST_RESULT_POOL))
 
         weigh(6)
-        release(2, 0)
-        release(2, 1)
         mx_group(5, 0)
-        release(3, 0)
-        release(3, 1)
+        for e, h in ((2, 0), (2, 1), (3, 0), (3, 1), (4, 0)):
+            release(e, h)
         mx_group(4, 1)
         sigmoid(7)
         add_embed(2, 0)
@@ -332,54 +314,49 @@ def tile_soft_dispatch_expert_inputs_g2_kernel(
         store_codes(0)
         add_embed(2, 1)
         store_y(2)
-        release(4, 0)
-        release(4, 1)
         mx_group(5, 1)
         mx_group(6, 0)
-        y_part("pool", 2)
+        y_interleave("pool", 2)
         finish(3)
+        release(4, 1)
         mx_group(6, 1)
-        y_part("pool", 3, slice(0, Y3_POOL))
-        finish(4)
+        y_interleave("pool", 3)
+        add_embed(4, 0)
 
         first, second = slice(0, P), slice(P, PAIR)
-        y_part("pool", 4, slice(0, Y4_POOL))
         weigh(7)
-        release(5, 0)
-        release(5, 1)
-        y_part("scalar", 3, slice(Y3_POOL, PAIR))
-        release(6, 0)
-        y_part("scalar", 4, slice(Y4_POOL, PAIR))
-        release(7, 0)
-        y_quantize(2, 2)
-        store_codes(2)
-        store_scales(0, [nc.sync])
+        for e, h in ((5, 0), (5, 1), (6, 0), (7, 0)):
+            release(e, h)
+        add_embed(4, 1)
+        store_y(4)
         d_quantize(7)
         mx_group(7, 0)
         mx_group(7, 1)
-        finish(5)
-        y_part("pool", 5, first)
-        y_part("scalar", 5, second)
+        y_interleave("scalar", 4)
+        y_quantize(2, 2)
+        store_codes(2)
+        store_scales(0, [nc.sync])
         for e in (6, 7):
             add_embed(e, 0)
             store_y(e, first)
-        release(6, 1)
-        release(7, 1)
+        for e in (6, 7):
+            y_interleave("scalar", e, first)
+            release(e, 1)
+        finish(5)
         y_quantize(4, 1)
-        y_quantize(5, 1)
-        store_codes(4)
-        y_part("vector", 6, first)
-        y_part("vector", 7, first)
         y_quantize_tile(6, 0)
-        add_embed(6, 1)
-        store_y(6, second)
-        y_part("scalar", 6, second)
         y_quantize_tile(7, 0)
         store_codes(6, first)
+        add_embed(6, 1)
+        store_y(6, second)
+        y_interleave("scalar", 5, second)
+        y_interleave("vector", 5, first)
         add_embed(7, 1)
         store_y(7, second)
-        y_part("scalar", 7, slice(P + LAST_VECTOR, PAIR))
-        y_part("vector", 7, slice(P, P + LAST_VECTOR))
+        y_interleave("scalar", 6, second)
+        y_quantize(5, 1)
+        store_codes(4)
+        y_interleave("vector", 7, second)
         y_quantize_tile(6, 1)
         y_quantize_tile(7, 1)
         store_codes(6, second)

from contextlib import ExitStack

import concourse.mybir as mybir
from concourse.masks import make_identity

T, D, S = 2048, 1024, 1024
FLOPS = 2 * T * D * S

F32 = mybir.dt.float32
BF16 = mybir.dt.bfloat16
I32 = mybir.dt.int32
U32 = mybir.dt.uint32
U8 = mybir.dt.uint8
FP8X4 = mybir.dt.float8_e4m3fn_x4
ACT = mybir.ActivationFunctionType
ALU = mybir.AluOpType

P = 128
PACK = 4
PASS = P * PACK
PASSES = T // PASS
HALF = 512
PAIR = 2 * P
TILES = S // P
EARLY_TILES = HALF // P
RUN = 4

SHORT_SHARE = 320
SCALAR_PIECE = 5
X_POOL = [0, SHORT_SHARE, SHORT_SHARE, SHORT_SHARE, SHORT_SHARE, 0, SHORT_SHARE, HALF]
FIRST_RESULT_POOL = 96

RESULTS = [(0, 0), (1, 0), (0, 1), (1, 1), (2, 0), (2, 1), (3, 0), (3, 1)]
BANK = [[0, 1, 2, 3, 1, 2, 5, 0], [4, 5, 6, 0, 3, 4, 6, 1]]
SCALED_BUFS = 6


def tile_soft_dispatch_expert_inputs_g2_kernel(
    tc, x, logits, token_weight, slot_scale, slot_embed, out_0, out_1, out_2
):
    nc = tc.nc
    with ExitStack() as ctx:
        sb = ctx.enter_context(tc.tile_pool(name="sb", bufs=1))
        ps = ctx.enter_context(tc.psum_pool(name="ps", bufs=1))

        def tiles(name, count, shape, dtype):
            return [sb.tile(shape, dtype, name="%s%d" % (name, n), align_bytes=64) for n in range(count)]

        banks = [ps.tile([P, HALF], F32, name="bank%d" % n) for n in range(7)]
        weight = ps.tile([P, P, PACK], F32, name="weight")
        ident = sb.tile([P, P], F32, name="ident", align_bytes=64)
        weight_raw = sb.tile([PASSES, PASS], BF16, name="weight_raw", align_bytes=64)
        factor_rows = sb.tile([P, PASS + P], F32, name="factor_rows", align_bytes=64)
        scale_raw = sb.tile([TILES, P], BF16, name="scale_raw", align_bytes=64)
        scale = sb.tile([P, TILES], F32, name="scale", align_bytes=64)
        logit_early = tiles("logit_early", PASSES, [P, PACK, HALF], BF16)
        logit_late = tiles("logit_late", 2, [P, PASSES, PACK, PAIR], BF16)
        x_raw = tiles("x_raw", 2 * PASSES, [P, PACK, HALF], BF16)
        embed = tiles("embed", 2, [P, PACK, S], BF16)
        gate = tiles("gate", 2, [P, HALF * PACK], F32)
        dispatch = tiles("dispatch", 2, [P, HALF * PACK], BF16)
        x_words = sb.tile([P, 2 * HALF, PACK], BF16, name="x_words", align_bytes=64)
        x_words_scalar = sb.tile([P, HALF, PACK], BF16, name="x_words_scalar", align_bytes=64)
        d_codes = tiles("d_codes", TILES, [P, HALF], U32)
        d_scales = tiles("d_scales", TILES, [P, HALF], U8)
        x_codes = tiles("x_codes", 2 * PASSES, [P, HALF], U32)
        x_scales = tiles("x_scales", 2 * PASSES, [P, HALF], U8)
        scaled = tiles("scaled", SCALED_BUFS, [P, PACK, P], F32)
        y = tiles("y", 2, [P, PACK, 2 * PAIR], F32)
        y_words = tiles("y_words", 2, [P, 2, PAIR, PACK], BF16)
        y_codes = tiles("y_codes", 3, [P, 2, PAIR], U32)
        y_scales = sb.tile([P, 2, S], U8, name="y_scales", align_bytes=64)

        ctx.enter_context(tc.manual_schedule())

        def rows(src, k, cols):
            return src[PASS * k : PASS * (k + 1), cols].rearrange("(p t) w -> p t w", t=PACK)

        nc.scalar.dma_start(out=weight_raw[:], in_=token_weight.rearrange("(k w) -> k w", k=PASSES))
        nc.scalar.dma_start(out=scale_raw[:], in_=slot_scale.rearrange("(i p) -> i p", p=P))
        nc.vector.memset(factor_rows[:], 0.0)

        def load_x(u):
            group = u // PASSES
            nc.sync.dma_start(out=x_raw[u][:], in_=rows(x, u % PASSES, slice(HALF * group, HALF * (group + 1))))

        def load_early(k):
            nc.sync.dma_start(out=logit_early[k][:], in_=rows(logits, k, slice(0, HALF)))

        def load_late(n):
            for k in range(PASSES):
                nc.sync.dma_start(
                    out=logit_late[n][:, k], in_=rows(logits, k, slice(HALF + PAIR * n, HALF + PAIR * (n + 1))))

        def load_embed(g, cols):
            nc.sync.dma_start(out=embed[g][:, :, cols], in_=rows(slot_embed, g, cols))

        load_early(0)
        load_x(0)
        for k in range(1, PASSES):
            load_x(k)
            load_early(k)
        load_x(4)
        load_late(0)
        load_x(5)
        load_x(6)
        load_embed(0, slice(0, HALF))
        load_x(7)
        load_late(1)
        load_embed(1, slice(0, S))
        load_embed(0, slice(HALF, S))

        make_identity(nc, ident[:])
        nc.vector.tensor_copy(out=factor_rows[0:PASSES, 0:PASS], in_=weight_raw[:])
        nc.vector.tensor_copy(out=factor_rows[0:TILES, PASS:], in_=scale_raw[:])
        for t in range(PACK):
            nc.tensor.transpose(weight[:, :, t], factor_rows[:, t:PASS:PACK], ident[:])
        nc.tensor.transpose(banks[6][:, 0:P], factor_rows[:, PASS:], ident[:])

        def interleave(engine, words, src, cols):
            dst, src = words[:, cols, :], src[:, :, cols]
            if engine == "pool":
                nc.gpsimd.tensor_scalar(
                    out=dst, in0=src.rearrange("p t c -> p c t"),
                    scalar1=1.0, scalar2=-0.0, op0=ALU.mult, op1=ALU.add)
                return
            dst = dst.rearrange("p (c i) t -> p c t i", i=RUN)
            src = src.rearrange("p t (c i) -> p c t i", i=RUN)
            if engine == "vector":
                nc.vector.tensor_copy(out=dst, in_=src)
            else:
                nc.scalar.copy(out=dst, in_=src)

        def x_window(u):
            rest = HALF - X_POOL[u]
            if u % 2 == 0:
                return x_words[:, HALF - rest : 2 * HALF - rest, :], slice(rest, HALF), slice(0, rest)
            return x_words[:, HALF:, :], slice(0, X_POOL[u]), slice(X_POOL[u], HALF)

        def x_pool(u):
            words, pool_cols, rest_cols = x_window(u)
            interleave("pool", words, x_raw[u], pool_cols)

        def x_rest(engine, u):
            words, pool_cols, rest_cols = x_window(u)
            interleave(engine, words, x_raw[u], rest_cols)

        def x_quantize(u):
            words = x_words_scalar[:] if u == SCALAR_PIECE else x_window(u)[0]
            nc.vector.quantize_mx(
                out=x_codes[u][:].bitcast(FP8X4), scales=x_scales[u][:], in_=words.rearrange("p c t -> p (c t)"))

        def sigmoid(n):
            if n < EARLY_TILES:
                dst = gate[n % 2][:].rearrange("p (s t) -> p s t", t=PACK)
                src = logit_early[n][:].rearrange("p t s -> p s t")
            else:
                cols = slice(P * (n % 2), P * (n % 2 + 1))
                dst = gate[n % 2][:].rearrange("p (k s t) -> p k s t", k=PASSES, t=PACK)
                src = logit_late[(n - EARLY_TILES) // 2][:, :, :, cols].rearrange("p k t s -> p k s t")
            nc.scalar.activation(out=dst, in_=src, func=ACT.Sigmoid)

        def weigh(n):
            count = 1 if n < EARLY_TILES else PASSES
            factor = weight[:, n : n + 1, :] if n < EARLY_TILES else weight[:, 0:PASSES, :]
            nc.vector.tensor_tensor(
                out=dispatch[n % 2][:].rearrange("p (k s t) -> p k s t", k=count, t=PACK),
                in0=gate[n % 2][:].rearrange("p (k s t) -> p k s t", k=count, t=PACK),
                in1=factor.unsqueeze(2).to_broadcast([P, count, HALF // count, PACK]), op=ALU.mult)

        def d_quantize(n):
            nc.vector.quantize_mx(out=d_codes[n][:].bitcast(FP8X4), scales=d_scales[n][:], in_=dispatch[n % 2][:])

        def mx_pass(i, g, k):
            n, block = (k, i) if i < EARLY_TILES else (i, k)
            cols = slice(P * block, P * (block + 1))
            nc.tensor.matmul_mx(
                out=banks[BANK[g][i]][:],
                lhsT=d_codes[n][:, cols].bitcast(FP8X4), lhsT_scale=d_scales[n][:, cols],
                rhs=x_codes[PASSES * g + k][:].bitcast(FP8X4), rhs_scale=x_scales[PASSES * g + k][:],
                start=(k == 0), stop=(k == PASSES - 1))

        def pass_over(slot_tiles, g, k):
            for i in slot_tiles:
                mx_pass(i, g, k)

        def mx_group(i, g):
            for k in range(PASSES):
                mx_pass(i, g, k)

        def y_of(e):
            return y[e // 2 % 2][:, :, PAIR * (e % 2) : PAIR * (e % 2 + 1)]

        def release(e, h):
            a, g = RESULTS[e]
            i = 2 * a + h
            bank, rows_t = banks[BANK[g][i]], scaled[(2 * e + h) % SCALED_BUFS]
            nc.scalar.activation(
                out=rows_t[:], in_=bank[:].rearrange("p (m t) -> p t m", t=PACK),
                func=ACT.Copy, scale=scale[:, i : i + 1])
            for t in range(PACK):
                nc.tensor.transpose(bank[:, P * t : P * (t + 1)], rows_t[:, t, :], ident[:])

        def add_embed(e, h):
            a, g = RESULTS[e]
            i = 2 * a + h
            nc.vector.tensor_tensor(
                out=y_of(e)[:, :, P * h : P * (h + 1)],
                in0=banks[BANK[g][i]][:].rearrange("p (t s) -> p t s", t=PACK),
                in1=embed[g][:, :, P * i : P * (i + 1)], op=ALU.add)

        def store_y(e, cols=slice(0, PAIR)):
            a, g = RESULTS[e]
            nc.sync.dma_start(
                out=rows(out_0, g, slice(PAIR * a + cols.start, PAIR * a + cols.stop)), in_=y_of(e)[:, :, cols])

        def finish(e):
            add_embed(e, 0)
            add_embed(e, 1)
            store_y(e)

        def y_interleave(engine, e, cols=slice(0, PAIR)):
            interleave(engine, y_words[e // 2 % 2][:, e % 2], y_of(e), cols)

        def y_quantize(e, count):
            a, g = RESULTS[e]
            held = slice(e % 2, e % 2 + count)
            nc.vector.quantize_mx(
                out=y_codes[e // 2 % 3][:, held, :].rearrange("p u m -> p (u m)").bitcast(FP8X4),
                scales=y_scales[:, g, PAIR * a : PAIR * (a + count)],
                in_=y_words[e // 2 % 2][:, held].rearrange("p u c t -> p (u c t)"))

        def y_quantize_tile(e, h):
            a, g = RESULTS[e]
            cols = slice(P * h, P * (h + 1))
            nc.vector.quantize_mx(
                out=y_codes[e // 2 % 3][:, e % 2, cols].bitcast(FP8X4),
                scales=y_scales[:, g, P * (2 * a + h) : P * (2 * a + h + 1)],
                in_=y_words[e // 2 % 2][:, e % 2, cols].rearrange("p c t -> p (c t)"))

        def store_codes(e, cols=slice(0, PAIR)):
            a, g = RESULTS[e]
            if RESULTS[e + 1][1] == g:
                dst = out_1[g, :, PAIR * a : PAIR * (a + 2), :].rearrange("p (u m) t -> p u (m t)", u=2)
            else:
                dst = out_1[:, :, PAIR * a + cols.start : PAIR * a + cols.stop, :].rearrange("g p m t -> p g (m t)")
            nc.sync.dma_start(out=dst.bitcast(I32), in_=y_codes[e // 2 % 3][:, :, cols].bitcast(I32))

        def store_scales(half, queues):
            cols = slice(HALF * half, HALF * (half + 1))
            for q in range(4):
                queues[q % len(queues)].dma_start(
                    out=out_2[:, 4 * q : 4 * q + 4, cols].rearrange("g r s -> r g s").bitcast(I32),
                    in_=y_scales[32 * q : 32 * q + 4, :, cols].bitcast(I32))

        sigmoid(0)
        x_rest("vector", 0)
        nc.scalar.copy(out=scale[:], in_=banks[6][:, 0:TILES])
        x_rest("scalar", 1)

        for n in range(PASSES):
            x_pool(n + 1)
            weigh(n)
            sigmoid(n + 1)
            if n == 0:
                x_quantize(0)
            x_quantize(n + 1)
            if n + 1 < PASSES:
                x_rest("scalar", n + 2)
            d_quantize(n)
            pass_over(range(EARLY_TILES), 0, n)


        x_rest("vector", 6)
        x_pool(6)
        weigh(4)
        pass_over(range(3), 1, 0)
        interleave("scalar", x_words_scalar[:], x_raw[SCALAR_PIECE], slice(0, HALF))
        release(0, 0)
        release(0, 1)
        sigmoid(5)
        x_quantize(5)
        pass_over(range(3), 1, 1)
        x_quantize(6)
        pass_over(range(3), 1, 2)
        d_quantize(4)
        x_pool(7)
        finish(0)
        for k in range(3):
            mx_pass(3, 1, k)

        weigh(5)
        release(1, 0)
        release(1, 1)
        mx_group(4, 0)
        sigmoid(6)
        y_interleave("scalar", 0, slice(FIRST_RESULT_POOL, PAIR))
        x_quantize(7)
        pass_over(range(EARLY_TILES), 1, 3)
        d_quantize(5)
        finish(1)
        y_interleave("pool", 1)
        y_interleave("pool", 0, slice(0, FIRST_RESULT_POOL))

        weigh(6)
        mx_group(5, 0)
        for e, h in ((2, 0), (2, 1), (3, 0), (3, 1), (4, 0)):
            release(e, h)
        mx_group(4, 1)
        sigmoid(7)
        add_embed(2, 0)
        d_quantize(6)
        y_quantize(0, 2)
        store_codes(0)
        add_embed(2, 1)
        store_y(2)
        mx_group(5, 1)
        mx_group(6, 0)
        y_interleave("pool", 2)
        finish(3)
        release(4, 1)
        mx_group(6, 1)
        y_interleave("pool", 3)
        add_embed(4, 0)

        first, second = slice(0, P), slice(P, PAIR)
        weigh(7)
        for e, h in ((5, 0), (5, 1), (6, 0), (7, 0)):
            release(e, h)
        add_embed(4, 1)
        store_y(4)
        d_quantize(7)
        mx_group(7, 0)
        mx_group(7, 1)
        y_interleave("scalar", 4)
        y_quantize(2, 2)
        store_codes(2)
        store_scales(0, [nc.sync])
        for e in (6, 7):
            add_embed(e, 0)
            store_y(e, first)
        for e in (6, 7):
            y_interleave("scalar", e, first)
            release(e, 1)
        finish(5)
        y_quantize(4, 1)
        y_quantize_tile(6, 0)
        y_quantize_tile(7, 0)
        store_codes(6, first)
        add_embed(6, 1)
        store_y(6, second)
        y_interleave("scalar", 5, second)
        y_interleave("vector", 5, first)
        add_embed(7, 1)
        store_y(7, second)
        y_interleave("scalar", 6, second)
        y_quantize(5, 1)
        store_codes(4)
        y_interleave("vector", 7, second)
        y_quantize_tile(6, 1)
        y_quantize_tile(7, 1)
        store_codes(6, second)
        store_scales(1, [nc.scalar, nc.sync])
